import numpy as np
import ml_dtypes


def mxq(x, axis, fmt="e4m3"):
    dtype, down = {"e4m3": (ml_dtypes.float8_e4m3fn, 7), "e5m2": (ml_dtypes.float8_e5m2, 14)}[fmt]
    v = np.moveaxis(np.asarray(x, np.float32).astype(ml_dtypes.bfloat16).astype(np.float64), axis, -1)
    blocks = v.reshape(v.shape[:-1] + (-1, 32))
    amax = np.abs(blocks).max(-1, keepdims=True)
    byte = np.maximum(np.where(amax > 0, np.frexp(amax)[1] - 1 + 127, 0) - down, 1)
    scale = np.exp2(byte - 127.0)
    codes = (blocks / scale).astype(np.float32).astype(dtype).astype(np.float64)
    return np.moveaxis((codes * scale).reshape(v.shape), -1, axis)


WIDE = False


def mx_kscale(k):
    if not WIDE:
        return np.ones(k)
    levels = np.array([10, -10, 5, -5, 0])
    if k % 512:
        return np.exp2(np.random.permutation(np.resize(levels, k // 32))).repeat(32)
    a = np.empty((k // 512, 16))
    for p in range(k // 512):
        a[p, :8] = np.random.permutation(np.resize(levels, 8))
        for g in range(8):
            far = levels[np.abs(levels - a[p, g]) >= 10]
            a[p, g + 8] = far[np.random.randint(len(far))]
    return np.exp2(a.ravel()).repeat(32)


def f64(x):
    return np.asarray(x).astype(np.float64)


def striped(idx):
    return np.tile(idx.reshape(-1, 16).T, (8, 1)).astype(np.uint16)


def unstriped(offs):
    return offs[:16].T.reshape(-1).astype(np.int64)


E2M1 = np.array([0.0, 0.5, 1.0, 1.5, 2.0, 3.0, 4.0, 6.0, -0.0, -0.5, -1.0, -1.5, -2.0, -3.0, -4.0, -6.0])


def pack_weight(w, fmt):
    k, n = w.shape
    w = f64(np.asarray(w, np.float32).astype(ml_dtypes.bfloat16)).reshape(k // 32, 32, n)
    amax = np.abs(w).max(1)
    if fmt == "e4m3":
        byte = np.frexp(amax)[1] - 1 + 127 - 7
    else:
        mant, ex = np.frexp(amax / 6.0)
        byte = np.where(mant > 0.5, ex, ex - 1) + 127
    byte = np.clip(np.where(amax > 0, byte, 1), 1, 254)
    scaled = (w * np.exp2(127.0 - byte)[:, None, :]).reshape(k, n).astype(np.float32)
    by_word = np.ascontiguousarray(scaled.reshape(k // 512, 128, 4, n).transpose(0, 1, 3, 2))
    if fmt == "e4m3":
        words = by_word.astype(ml_dtypes.float8_e4m3fn).view(np.uint8)
    else:
        c = by_word.astype(ml_dtypes.float4_e2m1fn).view(np.uint8) & 0xF
        words = (c[..., 0::2] | (c[..., 1::2] << 4)).reshape(k // 512, 128, 2 * n)
    return np.ascontiguousarray(words), np.ascontiguousarray(byte.astype(np.uint8).reshape(k // 512, 16, n))


def unpack_weight(words, scales, fmt):
    g, _, n = scales.shape
    words = np.ascontiguousarray(words).reshape(g, 128, n, -1)
    if fmt == "e4m3":
        vals = words.view(ml_dtypes.float8_e4m3fn).astype(np.float64)
    else:
        nib = np.empty((g, 128, n, 4), np.uint8)
        nib[..., 0::2] = words & 0xF
        nib[..., 1::2] = words >> 4
        vals = E2M1[nib]
    vals = vals * np.repeat(np.exp2(scales.astype(np.float64) - 127.0), 8, axis=1)[..., None]
    return vals.transpose(0, 1, 3, 2).reshape(g * 512, n)


def gelu(v):
    return 0.5 * v * (1.0 + np.tanh(np.sqrt(2.0 / np.pi) * (v + 0.044715 * v**3)))


K, K1, T, S, H, T2, P, N = 1536, 1024, 4096, 1024, 1024, 2048, 1024, 384

def setup_inputs():
    n = np.random.standard_normal
    s = mx_kscale(K)[:, None]
    u = mx_kscale(H)[:, None]
    tab_words, tab_scales = pack_weight(n((K, T)) * s, "e4m3")
    wh_words, wh_scales = pack_weight(n((K1, H)) / np.sqrt(K) / s[:K1], "e2m1")
    wb = (n((K - K1, H)) / np.sqrt(K) / s[K1:]).astype(np.float32)
    wo_words, wo_scales = pack_weight(n((H, N)) / np.sqrt(H) / u, "e4m3")
    return {
        "tab_words": tab_words, "tab_scales": tab_scales,
        "offs": striped(np.random.permutation(T)[:S]),
        "wh_words": wh_words, "wh_scales": wh_scales, "wb": wb,
        "gain": (np.exp(0.3 * n(H)) * u[:, 0]).astype(np.float32),
        "wgs": np.exp(0.3 * n((128, S))).astype(np.float32),
        "offs2": striped(np.random.permutation(T2)[:S]),
        "stock": (0.7 * n((H, T2)) * u).astype(np.float32),
        "wo_words": wo_words, "wo_scales": wo_scales,
        "offs3": striped(np.random.permutation(T2)[:P]),
        "cap": (0.4 + 0.4 * n(N)).astype(np.float32),
        "wgo": np.exp(0.3 * n((128, P))).astype(np.float32),
        "offs4": striped(np.random.permutation(T2)[:P]),
    }

def reference(tab_words, tab_scales, offs, wh_words, wh_scales, wb, gain, wgs, offs2, stock, wo_words, wo_scales, offs3, cap, wgo, offs4):
    v = unpack_weight(tab_words, tab_scales, "e4m3")[:, unstriped(offs)]
    wh = unpack_weight(wh_words, wh_scales, "e2m1")
    d = wh.T @ v[:K1] + mxq(f64(wb), 0, "e4m3").T @ v[K1:]
    h = f64(gain)[:, None] * np.tanh(d)
    page = np.zeros((H, T2))
    page[:, unstriped(offs2)] = np.tile(f64(wgs), (H // 128, 1)) * h
    z = page + f64(stock)
    wo = unpack_weight(wo_words, wo_scales, "e4m3")
    y = wo.T @ mxq(z, 0, "e4m3")
    x = np.minimum(y[:, unstriped(offs3)], f64(cap)[:, None])
    out = np.zeros((N, T2))
    out[:, unstriped(offs4)] = np.tile(f64(wgo), (N // 128, 1)) * x
    return out

@@ -1,0 +1,317 @@
+from contextlib import ExitStack
+
+import concourse.mybir as mybir
+from concourse.masks import make_identity
+
+F32 = mybir.dt.float32
+BF16 = mybir.dt.bfloat16
+I32 = mybir.dt.int32
+U32 = mybir.dt.uint32
+U16 = mybir.dt.uint16
+U8 = mybir.dt.uint8
+FP8X4 = mybir.dt.float8_e4m3fn_x4
+FP4X4 = mybir.dt.float4_e2m1fn_x4
+ACT = mybir.ActivationFunctionType
+ALU = mybir.AluOpType
+
+P = 128
+T, S, H, T2, N = 4096, 1024, 1024, 2048, 384
+BANK = 512
+KB = 1024
+FLOPS = 2 * (1536 * H * S + H * N * T2)
+
+EARLY = 256
+WB_PIECES = ((0, 256), (256, 512), (512, 1024))
+H_AT = {1: 52, 2: 48, 3: 56, 4: 60, 5: 32, 6: 36, 7: 40}
+X_AT = (44, 56, 60)
+OUT_AT = (64, 72, 48)
+
+
+def tile_list_pharmacy_slot_orders_kernel(
+    tc, tab_words, tab_scales, offs, wh_words, wh_scales, wb, gain, wgs, offs2, stock,
+    wo_words, wo_scales, offs3, cap, wgo, offs4, out,
+):
+    nc = tc.nc
+    with ExitStack() as ctx:
+        held = ctx.enter_context(tc.tile_pool(name="held", bufs=1))
+        shared = ctx.enter_context(tc.tile_pool(name="shared", bufs=1))
+        ring = ctx.enter_context(tc.tile_pool(name="ring", bufs=1))
+        psum = ctx.enter_context(tc.psum_pool(name="psum", bufs=1))
+
+        def psum_bank(name, b):
+            return psum.tile([P, BANK], F32, name=name, offset=2 * KB * b)
+
+        lists = [held.tile([P, S // 16], U16, name=f"list{i}") for i in range(4)]
+        table = [shared.tile([P, T], I32, name=f"table{a}", offset=16 * KB * a) for a in range(3)]
+        tscale = [shared.tile([P, T], U8, name=f"tscale{i}", offset=(72 + 4 * i) * KB) for i in range(2)]
+        widths = (EARLY, H - EARLY)
+        wh_sc = [held.tile([P, 2, w], U8, name=f"wh_sc{w}", align_bytes=64) for w in widths]
+        wh_w = [held.tile([P, 2, 2 * w], U8, name=f"wh_w{w}", align_bytes=64) for w in widths]
+        wo_sc = held.tile([P, 2, N], U8, name="wo_sc", align_bytes=64)
+        g_sc = [held.tile([P, S], U8, name=f"g_sc{i}", align_bytes=64) for i in range(2)]
+        g_w = [held.tile([P, S], U32, name=f"g_w{a}", align_bytes=64) for a in range(3)]
+        rows = held.tile([P, P], F32, name="rows")
+        ident = held.tile([P, P], F32, name="ident")
+        warm = held.tile([P, 1], F32, name="warm")
+
+        nc.vector.memset(tscale[0][:].bitcast(I32), 0)
+        nc.vector.memset(rows[:], 0.0)
+        nc.vector.memset(tscale[1][:].bitcast(I32), 0)
+        nc.vector.memset(wh_sc[0][:].rearrange("p a c -> p (a c)").bitcast(I32), 0)
+        nc.vector.memset(wh_sc[1][:].rearrange("p a c -> p (a c)").bitcast(I32), 0)
+        nc.vector.memset(wo_sc[:].rearrange("p a c -> p (a c)").bitcast(I32), 0)
+        make_identity(nc, ident[:])
+        pages = [held.tile([P, T2], F32, name=f"page{i}") for i in range(3)]
+        for page in pages:
+            nc.gpsimd.memset(page[:], 0.0)
+
+        def load_table(a):
+            nc.sync.dma_start(table[a][:], tab_words[a].rearrange("p t i -> p (t i)").bitcast(I32))
+
+        def load_scale_rows(queue, plane, scales):
+            for q in range(4):
+                queue.dma_start(
+                    plane[32 * q : 32 * q + 4, :, :].bitcast(I32),
+                    scales[:, 4 * q : 4 * q + 4, :].rearrange("a r c -> r a c"),
+                )
+
+        wb_raw, wb_codes, wb_sc = [], [], []
+
+        def load_wb(i):
+            c0, c1 = WB_PIECES[i]
+            raw = shared.tile([P, 4, c1 - c0], F32, name=f"wb_raw{i}", offset=48 * KB + 16 * c0)
+            nc.sync.dma_start(raw[:], wb[:, c0:c1].rearrange("(p j) c -> p j c", j=4))
+            wb_raw.append(raw)
+
+        def quantise_wb(i):
+            c0, c1 = WB_PIECES[i]
+            w = c1 - c0
+            grouped = shared.tile([P, w, 4], BF16, name=f"wb_bf{i}", offset=64 * KB + 8 * c0, align_bytes=64)
+            nc.scalar.copy(
+                grouped[:].rearrange("p (c i) j -> p c j i", i=4),
+                wb_raw[i][:].rearrange("p j (c i) -> p c j i", i=4),
+            )
+            codes = held.tile([P, w], U32, name=f"wb_codes{i}", align_bytes=64)
+            sc = held.tile([P, w], U8, name=f"wb_sc{i}", align_bytes=64)
+            nc.vector.quantize_mx(codes[:].bitcast(FP8X4), sc[:], grouped[:].rearrange("p c j -> p (c j)"))
+            wb_codes.append(codes)
+            wb_sc.append(sc)
+
+        ts32 = tab_scales.bitcast(I32)
+        whs32 = wh_scales.bitcast(I32)
+        wh32 = wh_words.bitcast(I32).rearrange("a p c -> p a c")
+        nc.scalar.activation(warm[:], rows[:, 0:1], ACT.Tanh)
+        load_table(0)
+        nc.sync.dma_start(lists[0][:], offs)
+        for q in range(4):
+            nc.sync.dma_start(tscale[0][32 * q : 32 * q + 8, :].bitcast(I32), ts32[0:3:2, 4 * q : 4 * q + 4, :])
+        load_table(1)
+        nc.sync.dma_start(rows[0:8, :], gain.rearrange("(c p) -> c p", p=P))
+        for q in range(4):
+            nc.sync.dma_start(tscale[1][32 * q : 32 * q + 4, :].bitcast(I32), ts32[1, 4 * q : 4 * q + 4, :])
+        load_wb(0)
+        load_table(2)
+        nc.sync.dma_start(wh_w[0][:].bitcast(I32), wh32[:, :, 0 : EARLY // 2])
+        load_scale_rows(nc.sync, wh_sc[0], whs32[:, :, 0 : EARLY // 4])
+        nc.sync.dma_start(lists[1][:], offs2)
+        wgs_sb = held.tile([P, S], F32, name="wgs_sb")
+        for half in range(2):
+            nc.sync.dma_start(wgs_sb[:, BANK * half : BANK * (half + 1)], wgs[:, BANK * half : BANK * (half + 1)])
+        load_wb(1)
+        nc.sync.dma_start(wh_w[1][:].bitcast(I32), wh32[:, :, EARLY // 2 : H // 2])
+        load_scale_rows(nc.sync, wh_sc[1], whs32[:, :, EARLY // 4 : H // 4])
+        load_wb(2)
+
+        gains = held.tile([P, 8], F32, name="gains")
+        turned = psum_bank("turned", 0)
+        nc.tensor.transpose(turned[:, 0:P], rows[:], ident[:])
+        nc.scalar.copy(gains[:], turned[:, 0:8])
+
+        for a in range(2):
+            nc.vector.tensor_copy(g_w[a][:], table[a][:].bitcast(U32).indirect(lists[0][:]))
+            nc.vector.tensor_copy(g_sc[a][:], tscale[a][:].indirect(lists[0][:]))
+        quantise_wb(0)
+        for half in range(2):
+            nc.vector.tensor_copy(
+                g_w[2][:, BANK * half : BANK * (half + 1)],
+                table[2][:].bitcast(U32).indirect(lists[0][:, 32 * half : 32 * (half + 1)]),
+            )
+
+        def first_stage(j):
+            if j == 0:
+                h = held.tile([P, S], F32, name="h0")
+                weights = held.tile([P, S], F32, name="wgs_gain")
+            else:
+                h = shared.tile([P, S], F32, name=f"h{j}", offset=H_AT[j] * KB)
+                weights = wgs_sb
+            piece = [i for i, (c0, c1) in enumerate(WB_PIECES) if c0 <= P * j < c1][0]
+            wcols = slice(P * j - WB_PIECES[piece][0], P * (j + 1) - WB_PIECES[piece][0])
+            late = int(P * j >= EARLY)
+            c0 = P * j - late * EARLY
+            for half in range(2):
+                js = slice(BANK * half, BANK * (half + 1))
+                d = psum_bank(f"d{j}_{half}", 4 + (2 * j + half) % 4)
+                for a in range(2):
+                    nc.tensor.matmul_mx(
+                        d[:],
+                        lhsT=wh_w[late][:, a, 2 * c0 : 2 * (c0 + P)].bitcast(FP4X4),
+                        lhsT_scale=wh_sc[late][:, a, c0 : c0 + P],
+                        rhs=g_w[a][:, js].bitcast(FP8X4),
+                        rhs_scale=g_sc[a][:, js],
+                        start=(a == 0),
+                        stop=False,
+                    )
+                nc.tensor.matmul_mx(
+                    d[:],
+                    lhsT=wb_codes[piece][:, wcols].bitcast(FP8X4),
+                    lhsT_scale=wb_sc[piece][:, wcols],
+                    rhs=g_w[2][:, js].bitcast(FP8X4),
+                    rhs_scale=g_sc[0][4:P, js],
+                    start=False,
+                    stop=True,
+                )
+                if j == 0:
+                    nc.scalar.activation(weights[:, js], wgs_sb[:, js], ACT.Copy, scale=gains[:, 0:1])
+                nc.scalar.activation(h[:, js], d[:], ACT.Tanh)
+            if j > 0:
+                nc.scalar.activation(h[:], h[:], ACT.Copy, scale=gains[:, j : j + 1])
+            return h, weights
+
+        def place(j, h, weights):
+            page = pages[j % 3]
+            if j == 0:
+                for half in range(2):
+                    js = slice(BANK * half, BANK * (half + 1))
+                    nc.vector.tensor_tensor(
+                        page[:].indirect(lists[1][:, 32 * half : 32 * (half + 1)]), h[:, js], weights[:, js], ALU.mult
+                    )
+            else:
+                nc.vector.tensor_tensor(page[:].indirect(lists[1][:]), h[:], weights[:], ALU.mult)
+
+        def load_stock(j):
+            st = ring.tile([P, T2], F32, name="st", tag="row", bufs=5)
+            nc.sync.dma_start(st[:], stock[P * j : P * (j + 1), :])
+            return st
+
+        zt = [
+            [shared.tile([P, 4 * BANK], BF16, name=f"zt{a}_{c}", offset=(16 * a + 4 * c) * KB) for c in range(4)]
+            for a in range(2)
+        ]
+
+        def copy_on(engine, dst, src):
+            if engine == "vector":
+                nc.vector.tensor_copy(dst, src)
+            else:
+                nc.scalar.copy(dst, src)
+
+        def turn(bank, src, c, first):
+            for b in range(4):
+                nc.tensor.matmul(
+                    bank[:, P * b : P * (b + 1)],
+                    lhsT=src[:, BANK * c + P * b : BANK * c + P * (b + 1)],
+                    rhs=ident[:],
+                    start=(first and b == 0),
+                    stop=(not first and b == 3),
+                    is_transpose=True,
+                )
+
+        def open_sum(j, first_bank):
+            st = load_stock(j)
+            banks = [psum_bank(f"zsum{j}_{c}", first_bank + c) for c in range(4)]
+            for c in range(4):
+                turn(banks[c], st, c, True)
+            return banks
+
+        def close_sum(j, banks, engines):
+            a, jq = divmod(j, 4)
+            for c in range(4):
+                turn(banks[c], pages[j % 3], c, False)
+                dst = zt[a][c][:].rearrange("t (b u g q e) -> t b u g q e", b=4, u=2, g=4, e=2)[:, :, :, jq, :, :]
+                copy_on(engines[c], dst, banks[c][:].rearrange("t (b q u e) -> t b u q e", b=4, u=2, e=2))
+
+        z_codes = [held.tile([P, T2], U32, name=f"z_codes{a}", align_bytes=64) for a in range(2)]
+        z_sc = [held.tile([P, T2], U8, name=f"z_sc{a}", align_bytes=64) for a in range(2)]
+
+        def quantise_z(a, c, engines):
+            words = zt[a][c][:].bitcast(F32).rearrange("t (b u p) -> t b u p", b=4, u=2)
+            zi = ring.tile([P, 4 * BANK], BF16, name="zi", tag="zi", bufs=3, align_bytes=64)
+            zw = zi[:].bitcast(F32).rearrange("p (h b t u) -> p h b t u", h=2, b=2, u=2)
+            for half in range(2):
+                bank = psum_bank(f"zback{a}_{c}_{half}", 4 + (2 * c + half) % 4)
+                view = bank[:].rearrange("p (b u t) -> p b u t", b=2, u=2)
+                for b in range(2):
+                    for u in range(2):
+                        nc.tensor.transpose(view[:, b, u, :], words[:, 2 * half + b, u, :], ident[:])
+                copy_on(engines[half], zw[:, half, :, :, :], view.rearrange("p b u t -> p b t u"))
+            cs = slice(BANK * c, BANK * (c + 1))
+            nc.vector.quantize_mx(z_codes[a][:, cs].bitcast(FP8X4), z_sc[a][:, cs], zi[:])
+
+        wo_w = held.tile([P, 2, N], I32, name="wo_w", align_bytes=64)
+
+        def second_pass(bank, n, c, a):
+            cs = slice(BANK * c, BANK * (c + 1))
+            nc.tensor.matmul_mx(
+                bank[:],
+                lhsT=wo_w[:, a, P * n : P * (n + 1)].bitcast(FP8X4),
+                lhsT_scale=wo_sc[:, a, P * n : P * (n + 1)],
+                rhs=z_codes[a][:, cs].bitcast(FP8X4),
+                rhs_scale=z_sc[a][:, cs],
+                start=(a == 0),
+                stop=(a == 1),
+            )
+
+        made = [first_stage(0)]
+        place(0, *made[0])
+        quantise_wb(1)
+        made.extend(first_stage(j) for j in (1, 2))
+        quantise_wb(2)
+        made.extend(first_stage(j) for j in range(3, 8))
+
+        scalar_only = ("scalar",) * 4
+        for j in range(6):
+            banks = open_sum(j, 0)
+            place(j + 1, *made[j + 1])
+            close_sum(j, banks, scalar_only)
+            if j == 2:
+                nc.sync.dma_start(wo_w[:], wo_words.rearrange("a p c i -> p a (c i)").bitcast(I32))
+                load_scale_rows(nc.sync, wo_sc, wo_scales.bitcast(I32))
+                nc.sync.dma_start(lists[2][:], offs3)
+                nc.sync.dma_start(lists[3][:], offs4)
+                wgo_sb = held.tile([P, S], F32, name="wgo_sb")
+                nc.sync.dma_start(wgo_sb[:], wgo)
+                caps = held.tile([P, 3], F32, name="caps")
+                with nc.allow_non_contiguous_dma(reason="one cap to a partition"):
+                    nc.sync.dma_start(caps[:], cap.rearrange("(c p) -> p c", p=P))
+                outs = [shared.tile([P, T2], F32, name=f"out{n}", offset=OUT_AT[n] * KB) for n in range(3)]
+                for o in outs:
+                    nc.gpsimd.memset(o[:], 0.0)
+            if j == 3:
+                for c in range(4):
+                    quantise_z(0, c, scalar_only)
+
+        banks6 = open_sum(6, 0)
+        banks7 = open_sum(7, 4)
+        place(7, *made[7])
+        close_sum(6, banks6, scalar_only)
+        ysum = [psum_bank(f"ysum0_{c}", c) for c in range(4)]
+        for c in range(4):
+            second_pass(ysum[c], 0, c, 0)
+        close_sum(7, banks7, ("scalar", "vector", "scalar", "vector"))
+        ys = [ring.tile([P, T2], F32, name="y", tag="row", bufs=5) for n in range(3)]
+        for c in range(4):
+            quantise_z(1, c, ("vector", "scalar"))
+            second_pass(ysum[c], 0, c, 1)
+            nc.scalar.copy(ys[0][:, BANK * c : BANK * (c + 1)], ysum[c][:])
+        for n in range(1, 3):
+            for c in range(4):
+                bank = psum_bank(f"ysum{n}_{c}", 4 * (n % 2) + c)
+                for a in range(2):
+                    second_pass(bank, n, c, a)
+                nc.scalar.copy(ys[n][:, BANK * c : BANK * (c + 1)], bank[:])
+
+        for n in range(3):
+            x = shared.tile([P, S], F32, name=f"x{n}", offset=X_AT[n] * KB)
+            nc.vector.tensor_copy(x[:], ys[n][:].indirect(lists[2][:]))
+            nc.vector.tensor_scalar(x[:], x[:], caps[:, n : n + 1], None, ALU.min)
+            nc.vector.tensor_tensor(outs[n][:].indirect(lists[3][:]), x[:], wgo_sb[:], ALU.mult)
+            nc.sync.dma_start(out[P * n : P * (n + 1), :], outs[n][:])

@@ -24,7 +24,6 @@ EARLY = 256
 WB_PIECES = ((0, 256), (256, 512), (512, 1024))
 H_AT = {1: 52, 2: 48, 3: 56, 4: 60, 5: 32, 6: 36, 7: 40}
 X_AT = (44, 56, 60)
-OUT_AT = (64, 72, 48)
 
 
 def tile_list_pharmacy_slot_orders_kernel(
@@ -62,8 +61,11 @@ def tile_list_pharmacy_slot_orders_kernel(
         nc.vector.memset(wo_sc[:].rearrange("p a c -> p (a c)").bitcast(I32), 0)
         make_identity(nc, ident[:])
         pages = [held.tile([P, T2], F32, name=f"page{i}") for i in range(3)]
-        for page in pages:
-            nc.gpsimd.memset(page[:], 0.0)
+        outs = {0: held.tile([P, T2], F32, name="out0")}
+        for window in pages[0:2]:
+            nc.gpsimd.memset(window[:].bitcast(I32), 0)
+        for window in (pages[2], outs[0]):
+            nc.vector.memset(window[:].bitcast(I32), 0)
 
         def load_table(a):
             nc.sync.dma_start(table[a][:], tab_words[a].rearrange("p t i -> p (t i)").bitcast(I32))
@@ -229,33 +231,57 @@ def tile_list_pharmacy_slot_orders_kernel(
                 dst = zt[a][c][:].rearrange("t (b u g q e) -> t b u g q e", b=4, u=2, g=4, e=2)[:, :, :, jq, :, :]
                 copy_on(engines[c], dst, banks[c][:].rearrange("t (b q u e) -> t b u q e", b=4, u=2, e=2))
 
-        z_codes = [held.tile([P, T2], U32, name=f"z_codes{a}", align_bytes=64) for a in range(2)]
+        z_codes = {}
+        z_lined = {}
         z_sc = [held.tile([P, T2], U8, name=f"z_sc{a}", align_bytes=64) for a in range(2)]
 
-        def quantise_z(a, c, engines):
+        def turn_back(a, c, engines):
             words = zt[a][c][:].bitcast(F32).rearrange("t (b u p) -> t b u p", b=4, u=2)
-            zi = ring.tile([P, 4 * BANK], BF16, name="zi", tag="zi", bufs=3, align_bytes=64)
-            zw = zi[:].bitcast(F32).rearrange("p (h b t u) -> p h b t u", h=2, b=2, u=2)
+            at = (64 * (1 - a) + 4 * c) * KB
+            if (a, c) == (1, 3):
+                parts = [
+                    shared.tile([P, 2 * BANK], BF16, name=f"zi_last{i}", offset=at + 2 * KB * i, align_bytes=64)
+                    for i in range(2)
+                ]
+                halves = [part[:] for part in parts]
+            else:
+                parts = [shared.tile([P, 4 * BANK], BF16, name=f"zi{a}_{c}", offset=at, align_bytes=64)]
+                halves = [parts[0][:, 2 * BANK * i : 2 * BANK * (i + 1)] for i in range(2)]
             for half in range(2):
-                bank = psum_bank(f"zback{a}_{c}_{half}", 4 + (2 * c + half) % 4)
+                bank = psum_bank(f"zback{a}_{c}_{half}", 4 * (1 - a) + (2 * c + half) % 4)
                 view = bank[:].rearrange("p (b u t) -> p b u t", b=2, u=2)
                 for b in range(2):
                     for u in range(2):
                         nc.tensor.transpose(view[:, b, u, :], words[:, 2 * half + b, u, :], ident[:])
-                copy_on(engines[half], zw[:, half, :, :, :], view.rearrange("p b u t -> p b t u"))
-            cs = slice(BANK * c, BANK * (c + 1))
-            nc.vector.quantize_mx(z_codes[a][:, cs].bitcast(FP8X4), z_sc[a][:, cs], zi[:])
+                dst = halves[half].bitcast(F32).rearrange("p (b t u) -> p b t u", b=2, u=2)
+                copy_on(engines[half], dst, view.rearrange("p b u t -> p b t u"))
+            z_lined[a, c] = parts
+
+        def quantise_z(a, c):
+            if a == 0 and c >= 2:
+                codes = shared.tile(
+                    [P, BANK], U32, name=f"z_codes{a}_{c}", offset=(H_AT[7] + 2 * (c - 2)) * KB, align_bytes=64
+                )
+            else:
+                codes = held.tile([P, BANK], U32, name=f"z_codes{a}_{c}", align_bytes=64)
+            w = BANK // len(z_lined[a, c])
+            for i, part in enumerate(z_lined[a, c]):
+                nc.vector.quantize_mx(
+                    codes[:, w * i : w * (i + 1)].bitcast(FP8X4),
+                    z_sc[a][:, BANK * c + w * i : BANK * c + w * (i + 1)],
+                    part[:],
+                )
+            z_codes[a, c] = codes
 
         wo_w = held.tile([P, 2, N], I32, name="wo_w", align_bytes=64)
 
-        def second_pass(bank, n, c, a):
-            cs = slice(BANK * c, BANK * (c + 1))
+        def second_pass(bank, n, c, a, c0=0, c1=BANK):
             nc.tensor.matmul_mx(
-                bank[:],
+                bank[:, c0:c1],
                 lhsT=wo_w[:, a, P * n : P * (n + 1)].bitcast(FP8X4),
                 lhsT_scale=wo_sc[:, a, P * n : P * (n + 1)],
-                rhs=z_codes[a][:, cs].bitcast(FP8X4),
-                rhs_scale=z_sc[a][:, cs],
+                rhs=z_codes[a, c][:, c0:c1].bitcast(FP8X4),
+                rhs_scale=z_sc[a][:, BANK * c + c0 : BANK * c + c1],
                 start=(a == 0),
                 stop=(a == 1),
             )
@@ -265,13 +291,15 @@ def tile_list_pharmacy_slot_orders_kernel(
         quantise_wb(1)
         made.extend(first_stage(j) for j in (1, 2))
         quantise_wb(2)
-        made.extend(first_stage(j) for j in range(3, 8))
+        made.append(first_stage(3))
 
         scalar_only = ("scalar",) * 4
-        for j in range(6):
+        for j in range(5):
             banks = open_sum(j, 0)
             place(j + 1, *made[j + 1])
             close_sum(j, banks, scalar_only)
+            if j < 3:
+                made.append(first_stage(j + 4))
             if j == 2:
                 nc.sync.dma_start(wo_w[:], wo_words.rearrange("a p c i -> p a (c i)").bitcast(I32))
                 load_scale_rows(nc.sync, wo_sc, wo_scales.bitcast(I32))
@@ -282,29 +310,45 @@ def tile_list_pharmacy_slot_orders_kernel(
                 caps = held.tile([P, 3], F32, name="caps")
                 with nc.allow_non_contiguous_dma(reason="one cap to a partition"):
                     nc.sync.dma_start(caps[:], cap.rearrange("(c p) -> p c", p=P))
-                outs = [shared.tile([P, T2], F32, name=f"out{n}", offset=OUT_AT[n] * KB) for n in range(3)]
-                for o in outs:
-                    nc.gpsimd.memset(o[:], 0.0)
             if j == 3:
                 for c in range(4):
-                    quantise_z(0, c, scalar_only)
+                    turn_back(0, c, scalar_only)
+                    if c < 2:
+                        quantise_z(0, c)
+                made.append(first_stage(7))
 
-        banks6 = open_sum(6, 0)
-        banks7 = open_sum(7, 4)
+        banks5 = open_sum(5, 0)
+        banks6 = open_sum(6, 4)
+        place(6, *made[6])
+        close_sum(5, banks5, scalar_only)
         place(7, *made[7])
+        for c in (2, 3):
+            quantise_z(0, c)
         close_sum(6, banks6, scalar_only)
-        ysum = [psum_bank(f"ysum0_{c}", c) for c in range(4)]
-        for c in range(4):
+        ysum = [psum_bank(f"ysum0_{c}", 4 + c) for c in range(4)]
+        for c in (0, 1):
             second_pass(ysum[c], 0, c, 0)
-        close_sum(7, banks7, ("scalar", "vector", "scalar", "vector"))
+        banks7 = open_sum(7, 0)
+        close_sum(7, banks7, ("scalar", "scalar", "vector", "scalar"))
         ys = [ring.tile([P, T2], F32, name="y", tag="row", bufs=5) for n in range(3)]
         for c in range(4):
-            quantise_z(1, c, ("vector", "scalar"))
+            turn_back(1, c, ("scalar" if c == 2 else "vector", "scalar"))
+            quantise_z(1, c)
+        for c in range(3):
+            if c >= 2:
+                second_pass(ysum[c], 0, c, 0)
             second_pass(ysum[c], 0, c, 1)
             nc.scalar.copy(ys[0][:, BANK * c : BANK * (c + 1)], ysum[c][:])
+        for i, bank in enumerate((ysum[3], psum_bank("ysum0_last", 0))):
+            c0, c1 = i * BANK // 2, (i + 1) * BANK // 2
+            for a in range(2):
+                second_pass(bank, 0, 3, a, c0, c1)
+            nc.scalar.copy(ys[0][:, 3 * BANK + c0 : 3 * BANK + c1], bank[:, c0:c1])
+        outs[1] = shared.tile([P, T2], F32, name="out1", offset=8 * KB)
+        nc.vector.memset(outs[1][:].bitcast(I32), 0)
         for n in range(1, 3):
             for c in range(4):
-                bank = psum_bank(f"ysum{n}_{c}", 4 * (n % 2) + c)
+                bank = psum_bank(f"ysum{n}_{c}", (4 * (n + 1) + c + 1) % 8)
                 for a in range(2):
                     second_pass(bank, n, c, a)
                 nc.scalar.copy(ys[n][:, BANK * c : BANK * (c + 1)], bank[:])
@@ -313,5 +357,5 @@ def tile_list_pharmacy_slot_orders_kernel(
             x = shared.tile([P, S], F32, name=f"x{n}", offset=X_AT[n] * KB)
             nc.vector.tensor_copy(x[:], ys[n][:].indirect(lists[2][:]))
             nc.vector.tensor_scalar(x[:], x[:], caps[:, n : n + 1], None, ALU.min)
-            nc.vector.tensor_tensor(outs[n][:].indirect(lists[3][:]), x[:], wgo_sb[:], ALU.mult)
-            nc.sync.dma_start(out[P * n : P * (n + 1), :], outs[n][:])
+            nc.vector.tensor_tensor(outs[n % 2][:].indirect(lists[3][:]), x[:], wgo_sb[:], ALU.mult)
+            nc.sync.dma_start(out[P * n : P * (n + 1), :], outs[n % 2][:])

@@ -22,8 +22,16 @@ FLOPS = 2 * (1536 * H * S + H * N * T2)
 
 EARLY = 256
 WB_PIECES = ((0, 256), (256, 512), (512, 1024))
+PAGES = 3
+ROW_BUFS = 5
+
+TABLE_AT = (0, 16, 32)
+WB_RAW_AT, WB_BF16_AT, TABLE_SCALES_AT = 48, 64, 72
 H_AT = {1: 52, 2: 48, 3: 56, 4: 60, 5: 32, 6: 36, 7: 40}
-X_AT = (44, 56, 60)
+Z_TURNED_AT = (0, 16)
+Z_LINED_AT = (64, 0)
+OUT1_AT = 8
+PICKED_AT = (44, 56, 60)
 
 
 def tile_list_pharmacy_slot_orders_kernel(
@@ -37,166 +45,169 @@ def tile_list_pharmacy_slot_orders_kernel(
         ring = ctx.enter_context(tc.tile_pool(name="ring", bufs=1))
         psum = ctx.enter_context(tc.psum_pool(name="psum", bufs=1))
 
-        def psum_bank(name, b):
-            return psum.tile([P, BANK], F32, name=name, offset=2 * KB * b)
+        def psum_bank(name, number):
+            return psum.tile([P, BANK], F32, name=name, offset=2 * KB * number)
+
+        def half_cols(half):
+            return slice(BANK * half, BANK * (half + 1))
+
+        def half_list(offsets, half):
+            return offsets[:, 32 * half : 32 * (half + 1)]
 
         lists = [held.tile([P, S // 16], U16, name=f"list{i}") for i in range(4)]
-        table = [shared.tile([P, T], I32, name=f"table{a}", offset=16 * KB * a) for a in range(3)]
-        tscale = [shared.tile([P, T], U8, name=f"tscale{i}", offset=(72 + 4 * i) * KB) for i in range(2)]
+        table = [shared.tile([P, T], I32, name=f"table{a}", offset=TABLE_AT[a] * KB) for a in range(3)]
+        table_sc = [
+            shared.tile([P, T], U8, name=f"table_sc{i}", offset=(TABLE_SCALES_AT + 4 * i) * KB) for i in range(2)
+        ]
         widths = (EARLY, H - EARLY)
         wh_sc = [held.tile([P, 2, w], U8, name=f"wh_sc{w}", align_bytes=64) for w in widths]
         wh_w = [held.tile([P, 2, 2 * w], U8, name=f"wh_w{w}", align_bytes=64) for w in widths]
         wo_sc = held.tile([P, 2, N], U8, name="wo_sc", align_bytes=64)
-        g_sc = [held.tile([P, S], U8, name=f"g_sc{i}", align_bytes=64) for i in range(2)]
-        g_w = [held.tile([P, S], U32, name=f"g_w{a}", align_bytes=64) for a in range(3)]
-        rows = held.tile([P, P], F32, name="rows")
+        picked_sc = [held.tile([P, S], U8, name=f"picked_sc{i}", align_bytes=64) for i in range(2)]
+        picked_w = [held.tile([P, S], U32, name=f"picked_w{a}", align_bytes=64) for a in range(3)]
+        gain_rows = held.tile([P, P], F32, name="gain_rows")
         ident = held.tile([P, P], F32, name="ident")
-        warm = held.tile([P, 1], F32, name="warm")
 
-        nc.vector.memset(tscale[0][:].bitcast(I32), 0)
-        nc.vector.memset(rows[:], 0.0)
-        nc.vector.memset(tscale[1][:].bitcast(I32), 0)
+        nc.vector.memset(table_sc[0][:].bitcast(I32), 0)
+        nc.vector.memset(gain_rows[:], 0.0)
+        nc.vector.memset(table_sc[1][:].bitcast(I32), 0)
         nc.vector.memset(wh_sc[0][:].rearrange("p a c -> p (a c)").bitcast(I32), 0)
         nc.vector.memset(wh_sc[1][:].rearrange("p a c -> p (a c)").bitcast(I32), 0)
         nc.vector.memset(wo_sc[:].rearrange("p a c -> p (a c)").bitcast(I32), 0)
         make_identity(nc, ident[:])
-        pages = [held.tile([P, T2], F32, name=f"page{i}") for i in range(3)]
-        outs = {0: held.tile([P, T2], F32, name="out0")}
+        pages = [held.tile([P, T2], F32, name=f"page{i}") for i in range(PAGES)]
+        out_windows = [held.tile([P, T2], F32, name="out0")]
         for window in pages[0:2]:
             nc.gpsimd.memset(window[:].bitcast(I32), 0)
-        for window in (pages[2], outs[0]):
+        for window in (pages[2], out_windows[0]):
             nc.vector.memset(window[:].bitcast(I32), 0)
 
         def load_table(a):
             nc.sync.dma_start(table[a][:], tab_words[a].rearrange("p t i -> p (t i)").bitcast(I32))
 
-        def load_scale_rows(queue, plane, scales):
+        def load_scale_rows(planes, scales):
             for q in range(4):
-                queue.dma_start(
-                    plane[32 * q : 32 * q + 4, :, :].bitcast(I32),
+                nc.sync.dma_start(
+                    planes[32 * q : 32 * q + 4, :, :].bitcast(I32),
                     scales[:, 4 * q : 4 * q + 4, :].rearrange("a r c -> r a c"),
                 )
 
         wb_raw, wb_codes, wb_sc = [], [], []
 
-        def load_wb(i):
-            c0, c1 = WB_PIECES[i]
-            raw = shared.tile([P, 4, c1 - c0], F32, name=f"wb_raw{i}", offset=48 * KB + 16 * c0)
-            nc.sync.dma_start(raw[:], wb[:, c0:c1].rearrange("(p j) c -> p j c", j=4))
+        def load_wb(piece):
+            c0, c1 = WB_PIECES[piece]
+            raw = shared.tile([P, 4, c1 - c0], F32, name=f"wb_raw{piece}", offset=WB_RAW_AT * KB + 16 * c0)
+            nc.sync.dma_start(raw[:], wb[:, c0:c1].rearrange("(p i) c -> p i c", i=4))
             wb_raw.append(raw)
 
-        def quantise_wb(i):
-            c0, c1 = WB_PIECES[i]
-            w = c1 - c0
-            grouped = shared.tile([P, w, 4], BF16, name=f"wb_bf{i}", offset=64 * KB + 8 * c0, align_bytes=64)
-            nc.scalar.copy(
-                grouped[:].rearrange("p (c i) j -> p c j i", i=4),
-                wb_raw[i][:].rearrange("p j (c i) -> p c j i", i=4),
+        def quantise_wb(piece):
+            c0, c1 = WB_PIECES[piece]
+            width = c1 - c0
+            lined = shared.tile(
+                [P, width, 4], BF16, name=f"wb_bf16_{piece}", offset=WB_BF16_AT * KB + 8 * c0, align_bytes=64
             )
-            codes = held.tile([P, w], U32, name=f"wb_codes{i}", align_bytes=64)
-            sc = held.tile([P, w], U8, name=f"wb_sc{i}", align_bytes=64)
-            nc.vector.quantize_mx(codes[:].bitcast(FP8X4), sc[:], grouped[:].rearrange("p c j -> p (c j)"))
+            nc.scalar.copy(
+                lined[:].rearrange("p (c e) i -> p c i e", e=4),
+                wb_raw[piece][:].rearrange("p i (c e) -> p c i e", e=4),
+            )
+            codes = held.tile([P, width], U32, name=f"wb_codes{piece}", align_bytes=64)
+            scales = held.tile([P, width], U8, name=f"wb_sc{piece}", align_bytes=64)
+            nc.vector.quantize_mx(codes[:].bitcast(FP8X4), scales[:], lined[:].rearrange("p c i -> p (c i)"))
             wb_codes.append(codes)
-            wb_sc.append(sc)
+            wb_sc.append(scales)
 
         ts32 = tab_scales.bitcast(I32)
         whs32 = wh_scales.bitcast(I32)
         wh32 = wh_words.bitcast(I32).rearrange("a p c -> p a c")
-        nc.scalar.activation(warm[:], rows[:, 0:1], ACT.Tanh)
-        load_table(0)
         nc.sync.dma_start(lists[0][:], offs)
-        for q in range(4):
-            nc.sync.dma_start(tscale[0][32 * q : 32 * q + 8, :].bitcast(I32), ts32[0:3:2, 4 * q : 4 * q + 4, :])
-        load_table(1)
-        nc.sync.dma_start(rows[0:8, :], gain.rearrange("(c p) -> c p", p=P))
-        for q in range(4):
-            nc.sync.dma_start(tscale[1][32 * q : 32 * q + 4, :].bitcast(I32), ts32[1, 4 * q : 4 * q + 4, :])
-        load_wb(0)
-        load_table(2)
-        nc.sync.dma_start(wh_w[0][:].bitcast(I32), wh32[:, :, 0 : EARLY // 2])
-        load_scale_rows(nc.sync, wh_sc[0], whs32[:, :, 0 : EARLY // 4])
         nc.sync.dma_start(lists[1][:], offs2)
+        load_table(2)
+        for q in range(4):
+            nc.sync.dma_start(table_sc[0][32 * q : 32 * q + 8, :].bitcast(I32), ts32[0:3:2, 4 * q : 4 * q + 4, :])
+        nc.sync.dma_start(gain_rows[0:8, :], gain.rearrange("(j p) -> j p", p=P))
+        load_table(0)
+        for q in range(4):
+            nc.sync.dma_start(table_sc[1][32 * q : 32 * q + 4, :].bitcast(I32), ts32[1, 4 * q : 4 * q + 4, :])
+        load_wb(0)
+        load_table(1)
+        nc.sync.dma_start(wh_w[0][:].bitcast(I32), wh32[:, :, 0 : EARLY // 2])
+        load_scale_rows(wh_sc[0], whs32[:, :, 0 : EARLY // 4])
         wgs_sb = held.tile([P, S], F32, name="wgs_sb")
         for half in range(2):
-            nc.sync.dma_start(wgs_sb[:, BANK * half : BANK * (half + 1)], wgs[:, BANK * half : BANK * (half + 1)])
+            nc.sync.dma_start(wgs_sb[:, half_cols(half)], wgs[:, half_cols(half)])
         load_wb(1)
         nc.sync.dma_start(wh_w[1][:].bitcast(I32), wh32[:, :, EARLY // 2 : H // 2])
-        load_scale_rows(nc.sync, wh_sc[1], whs32[:, :, EARLY // 4 : H // 4])
+        load_scale_rows(wh_sc[1], whs32[:, :, EARLY // 4 : H // 4])
         load_wb(2)
 
         gains = held.tile([P, 8], F32, name="gains")
-        turned = psum_bank("turned", 0)
-        nc.tensor.transpose(turned[:, 0:P], rows[:], ident[:])
-        nc.scalar.copy(gains[:], turned[:, 0:8])
+        gain_turned = psum_bank("gain_turned", 0)
+        nc.tensor.transpose(gain_turned[:, 0:P], gain_rows[:], ident[:])
+        nc.scalar.activation(gains[:], gain_turned[:, 0:8], ACT.Copy)
 
-        for a in range(2):
-            nc.vector.tensor_copy(g_w[a][:], table[a][:].bitcast(U32).indirect(lists[0][:]))
-            nc.vector.tensor_copy(g_sc[a][:], tscale[a][:].indirect(lists[0][:]))
+        for i, a in enumerate((2, 0)):
+            nc.vector.tensor_copy(picked_w[a][:], table[a][:].bitcast(U32).indirect(lists[0][:]))
+            nc.vector.tensor_copy(picked_sc[i][:], table_sc[i][:].indirect(lists[0][:]))
         quantise_wb(0)
         for half in range(2):
             nc.vector.tensor_copy(
-                g_w[2][:, BANK * half : BANK * (half + 1)],
-                table[2][:].bitcast(U32).indirect(lists[0][:, 32 * half : 32 * (half + 1)]),
+                picked_w[1][:, half_cols(half)], table[1][:].bitcast(U32).indirect(half_list(lists[0], half))
             )
 
         def first_stage(j):
             if j == 0:
                 h = held.tile([P, S], F32, name="h0")
-                weights = held.tile([P, S], F32, name="wgs_gain")
             else:
                 h = shared.tile([P, S], F32, name=f"h{j}", offset=H_AT[j] * KB)
-                weights = wgs_sb
             piece = [i for i, (c0, c1) in enumerate(WB_PIECES) if c0 <= P * j < c1][0]
-            wcols = slice(P * j - WB_PIECES[piece][0], P * (j + 1) - WB_PIECES[piece][0])
+            wb_cols = slice(P * j - WB_PIECES[piece][0], P * (j + 1) - WB_PIECES[piece][0])
             late = int(P * j >= EARLY)
-            c0 = P * j - late * EARLY
+            wh_col = P * j - late * EARLY
             for half in range(2):
-                js = slice(BANK * half, BANK * (half + 1))
+                js = half_cols(half)
                 d = psum_bank(f"d{j}_{half}", 4 + (2 * j + half) % 4)
+                nc.tensor.matmul_mx(
+                    d[:],
+                    lhsT=wb_codes[piece][:, wb_cols].bitcast(FP8X4),
+                    lhsT_scale=wb_sc[piece][:, wb_cols],
+                    rhs=picked_w[2][:, js].bitcast(FP8X4),
+                    rhs_scale=picked_sc[0][4:P, js],
+                    start=True,
+                    stop=False,
+                )
                 for a in range(2):
                     nc.tensor.matmul_mx(
                         d[:],
-                        lhsT=wh_w[late][:, a, 2 * c0 : 2 * (c0 + P)].bitcast(FP4X4),
-                        lhsT_scale=wh_sc[late][:, a, c0 : c0 + P],
-                        rhs=g_w[a][:, js].bitcast(FP8X4),
-                        rhs_scale=g_sc[a][:, js],
-                        start=(a == 0),
-                        stop=False,
+                        lhsT=wh_w[late][:, a, 2 * wh_col : 2 * (wh_col + P)].bitcast(FP4X4),
+                        lhsT_scale=wh_sc[late][:, a, wh_col : wh_col + P],
+                        rhs=picked_w[a][:, js].bitcast(FP8X4),
+                        rhs_scale=picked_sc[a][:, js],
+                        start=False,
+                        stop=(a == 1),
                     )
-                nc.tensor.matmul_mx(
-                    d[:],
-                    lhsT=wb_codes[piece][:, wcols].bitcast(FP8X4),
-                    lhsT_scale=wb_sc[piece][:, wcols],
-                    rhs=g_w[2][:, js].bitcast(FP8X4),
-                    rhs_scale=g_sc[0][4:P, js],
-                    start=False,
-                    stop=True,
-                )
-                if j == 0:
-                    nc.scalar.activation(weights[:, js], wgs_sb[:, js], ACT.Copy, scale=gains[:, 0:1])
                 nc.scalar.activation(h[:, js], d[:], ACT.Tanh)
-            if j > 0:
-                nc.scalar.activation(h[:], h[:], ACT.Copy, scale=gains[:, j : j + 1])
-            return h, weights
+            scaled = h[:, BANK:S] if j == 0 else h[:]
+            nc.scalar.activation(scaled, scaled, ACT.Copy, scale=gains[:, j : j + 1])
+            return h
 
-        def place(j, h, weights):
-            page = pages[j % 3]
+        wgs_gain = held.tile([P, BANK], F32, name="wgs_gain")
+        nc.scalar.activation(wgs_gain[:], wgs_sb[:, 0:BANK], ACT.Copy, scale=gains[:, 0:1])
+
+        def place(j, h):
+            page = pages[j % PAGES]
             if j == 0:
-                for half in range(2):
-                    js = slice(BANK * half, BANK * (half + 1))
+                for half, weights in enumerate((wgs_gain[:], wgs_sb[:, BANK:S])):
                     nc.vector.tensor_tensor(
-                        page[:].indirect(lists[1][:, 32 * half : 32 * (half + 1)]), h[:, js], weights[:, js], ALU.mult
+                        page[:].indirect(half_list(lists[1], half)), h[:, half_cols(half)], weights, ALU.mult
                     )
             else:
-                nc.vector.tensor_tensor(page[:].indirect(lists[1][:]), h[:], weights[:], ALU.mult)
+                nc.vector.tensor_tensor(page[:].indirect(lists[1][:]), h[:], wgs_sb[:], ALU.mult)
 
-        def load_stock(j):
-            st = ring.tile([P, T2], F32, name="st", tag="row", bufs=5)
-            nc.sync.dma_start(st[:], stock[P * j : P * (j + 1), :])
-            return st
-
-        zt = [
-            [shared.tile([P, 4 * BANK], BF16, name=f"zt{a}_{c}", offset=(16 * a + 4 * c) * KB) for c in range(4)]
+        z_turned = [
+            [
+                shared.tile([P, 4 * BANK], BF16, name=f"z_turned{a}_{c}", offset=(Z_TURNED_AT[a] + 4 * c) * KB)
+                for c in range(4)
+            ]
             for a in range(2)
         ]
 
@@ -206,46 +217,49 @@ def tile_list_pharmacy_slot_orders_kernel(
             else:
                 nc.scalar.copy(dst, src)
 
-        def turn(bank, src, c, first):
+        def turn(bank, src, c, opens):
             for b in range(4):
                 nc.tensor.matmul(
                     bank[:, P * b : P * (b + 1)],
                     lhsT=src[:, BANK * c + P * b : BANK * c + P * (b + 1)],
                     rhs=ident[:],
-                    start=(first and b == 0),
-                    stop=(not first and b == 3),
+                    start=(opens and b == 0),
+                    stop=(not opens and b == 3),
                     is_transpose=True,
                 )
 
         def open_sum(j, first_bank):
-            st = load_stock(j)
+            stock_sb = ring.tile([P, T2], F32, name="stock_sb", tag="row", bufs=ROW_BUFS)
+            nc.sync.dma_start(stock_sb[:], stock[P * j : P * (j + 1), :])
             banks = [psum_bank(f"zsum{j}_{c}", first_bank + c) for c in range(4)]
             for c in range(4):
-                turn(banks[c], st, c, True)
+                turn(banks[c], stock_sb, c, True)
             return banks
 
         def close_sum(j, banks, engines):
-            a, jq = divmod(j, 4)
+            a, g = divmod(j, 4)
             for c in range(4):
-                turn(banks[c], pages[j % 3], c, False)
-                dst = zt[a][c][:].rearrange("t (b u g q e) -> t b u g q e", b=4, u=2, g=4, e=2)[:, :, :, jq, :, :]
-                copy_on(engines[c], dst, banks[c][:].rearrange("t (b q u e) -> t b u q e", b=4, u=2, e=2))
+                turn(banks[c], pages[j % PAGES], c, False)
+                dst = z_turned[a][c][:].rearrange("t (b u g q e) -> t b u g q e", b=4, u=2, g=4, e=2)
+                copy_on(
+                    engines[c], dst[:, :, :, g, :, :], banks[c][:].rearrange("t (b q u e) -> t b u q e", b=4, u=2, e=2)
+                )
 
         z_codes = {}
         z_lined = {}
         z_sc = [held.tile([P, T2], U8, name=f"z_sc{a}", align_bytes=64) for a in range(2)]
 
         def turn_back(a, c, engines):
-            words = zt[a][c][:].bitcast(F32).rearrange("t (b u p) -> t b u p", b=4, u=2)
-            at = (64 * (1 - a) + 4 * c) * KB
+            words = z_turned[a][c][:].bitcast(F32).rearrange("t (b u p) -> t b u p", b=4, u=2)
+            at = (Z_LINED_AT[a] + 4 * c) * KB
             if (a, c) == (1, 3):
                 parts = [
-                    shared.tile([P, 2 * BANK], BF16, name=f"zi_last{i}", offset=at + 2 * KB * i, align_bytes=64)
+                    shared.tile([P, 2 * BANK], BF16, name=f"z_lined_last{i}", offset=at + 2 * KB * i, align_bytes=64)
                     for i in range(2)
                 ]
                 halves = [part[:] for part in parts]
             else:
-                parts = [shared.tile([P, 4 * BANK], BF16, name=f"zi{a}_{c}", offset=at, align_bytes=64)]
+                parts = [shared.tile([P, 4 * BANK], BF16, name=f"z_lined{a}_{c}", offset=at, align_bytes=64)]
                 halves = [parts[0][:, 2 * BANK * i : 2 * BANK * (i + 1)] for i in range(2)]
             for half in range(2):
                 bank = psum_bank(f"zback{a}_{c}_{half}", 4 * (1 - a) + (2 * c + half) % 4)
@@ -264,18 +278,18 @@ def tile_list_pharmacy_slot_orders_kernel(
                 )
             else:
                 codes = held.tile([P, BANK], U32, name=f"z_codes{a}_{c}", align_bytes=64)
-            w = BANK // len(z_lined[a, c])
+            width = BANK // len(z_lined[a, c])
             for i, part in enumerate(z_lined[a, c]):
                 nc.vector.quantize_mx(
-                    codes[:, w * i : w * (i + 1)].bitcast(FP8X4),
-                    z_sc[a][:, BANK * c + w * i : BANK * c + w * (i + 1)],
+                    codes[:, width * i : width * (i + 1)].bitcast(FP8X4),
+                    z_sc[a][:, BANK * c + width * i : BANK * c + width * (i + 1)],
                     part[:],
                 )
             z_codes[a, c] = codes
 
         wo_w = held.tile([P, 2, N], I32, name="wo_w", align_bytes=64)
 
-        def second_pass(bank, n, c, a, c0=0, c1=BANK):
+        def second_stage(bank, n, c, a, c0=0, c1=BANK):
             nc.tensor.matmul_mx(
                 bank[:, c0:c1],
                 lhsT=wo_w[:, a, P * n : P * (n + 1)].bitcast(FP8X4),
@@ -286,76 +300,78 @@ def tile_list_pharmacy_slot_orders_kernel(
                 stop=(a == 1),
             )
 
-        made = [first_stage(0)]
-        place(0, *made[0])
+        hs = [first_stage(0)]
+        place(0, hs[0])
         quantise_wb(1)
-        made.extend(first_stage(j) for j in (1, 2))
+        hs.extend(first_stage(j) for j in (1, 2))
         quantise_wb(2)
-        made.append(first_stage(3))
+        hs.append(first_stage(3))
 
         scalar_only = ("scalar",) * 4
         for j in range(5):
             banks = open_sum(j, 0)
-            place(j + 1, *made[j + 1])
+            place(j + 1, hs[j + 1])
             close_sum(j, banks, scalar_only)
             if j < 3:
-                made.append(first_stage(j + 4))
+                hs.append(first_stage(j + 4))
             if j == 2:
                 nc.sync.dma_start(wo_w[:], wo_words.rearrange("a p c i -> p a (c i)").bitcast(I32))
-                load_scale_rows(nc.sync, wo_sc, wo_scales.bitcast(I32))
+                load_scale_rows(wo_sc, wo_scales.bitcast(I32))
                 nc.sync.dma_start(lists[2][:], offs3)
                 nc.sync.dma_start(lists[3][:], offs4)
                 wgo_sb = held.tile([P, S], F32, name="wgo_sb")
                 nc.sync.dma_start(wgo_sb[:], wgo)
                 caps = held.tile([P, 3], F32, name="caps")
                 with nc.allow_non_contiguous_dma(reason="one cap to a partition"):
-                    nc.sync.dma_start(caps[:], cap.rearrange("(c p) -> p c", p=P))
+                    nc.sync.dma_start(caps[:], cap.rearrange("(n p) -> p n", p=P))
             if j == 3:
                 for c in range(4):
                     turn_back(0, c, scalar_only)
                     if c < 2:
                         quantise_z(0, c)
-                made.append(first_stage(7))
+                hs.append(first_stage(7))
 
         banks5 = open_sum(5, 0)
         banks6 = open_sum(6, 4)
-        place(6, *made[6])
+        place(6, hs[6])
         close_sum(5, banks5, scalar_only)
-        place(7, *made[7])
+        place(7, hs[7])
         for c in (2, 3):
             quantise_z(0, c)
         close_sum(6, banks6, scalar_only)
         ysum = [psum_bank(f"ysum0_{c}", 4 + c) for c in range(4)]
         for c in (0, 1):
-            second_pass(ysum[c], 0, c, 0)
+            second_stage(ysum[c], 0, c, 0)
         banks7 = open_sum(7, 0)
+
         close_sum(7, banks7, ("scalar", "scalar", "vector", "scalar"))
-        ys = [ring.tile([P, T2], F32, name="y", tag="row", bufs=5) for n in range(3)]
+        ys = [ring.tile([P, T2], F32, name="y", tag="row", bufs=ROW_BUFS) for n in range(3)]
         for c in range(4):
             turn_back(1, c, ("scalar" if c == 2 else "vector", "scalar"))
             quantise_z(1, c)
         for c in range(3):
-            if c >= 2:
-                second_pass(ysum[c], 0, c, 0)
-            second_pass(ysum[c], 0, c, 1)
+            if c == 2:
+                second_stage(ysum[c], 0, c, 0)
+            second_stage(ysum[c], 0, c, 1)
             nc.scalar.copy(ys[0][:, BANK * c : BANK * (c + 1)], ysum[c][:])
         for i, bank in enumerate((ysum[3], psum_bank("ysum0_last", 0))):
             c0, c1 = i * BANK // 2, (i + 1) * BANK // 2
             for a in range(2):
-                second_pass(bank, 0, 3, a, c0, c1)
+                second_stage(bank, 0, 3, a, c0, c1)
             nc.scalar.copy(ys[0][:, 3 * BANK + c0 : 3 * BANK + c1], bank[:, c0:c1])
-        outs[1] = shared.tile([P, T2], F32, name="out1", offset=8 * KB)
-        nc.vector.memset(outs[1][:].bitcast(I32), 0)
+        out_windows.append(shared.tile([P, T2], F32, name="out1", offset=OUT1_AT * KB))
+        nc.vector.memset(out_windows[1][:].bitcast(I32), 0)
         for n in range(1, 3):
             for c in range(4):
-                bank = psum_bank(f"ysum{n}_{c}", (4 * (n + 1) + c + 1) % 8)
+                bank = psum_bank(f"ysum{n}_{c}", (4 * (n - 1) + c + 1) % 8)
                 for a in range(2):
-                    second_pass(bank, n, c, a)
+                    second_stage(bank, n, c, a)
                 nc.scalar.copy(ys[n][:, BANK * c : BANK * (c + 1)], bank[:])
 
         for n in range(3):
-            x = shared.tile([P, S], F32, name=f"x{n}", offset=X_AT[n] * KB)
-            nc.vector.tensor_copy(x[:], ys[n][:].indirect(lists[2][:]))
-            nc.vector.tensor_scalar(x[:], x[:], caps[:, n : n + 1], None, ALU.min)
-            nc.vector.tensor_tensor(outs[n % 2][:].indirect(lists[3][:]), x[:], wgo_sb[:], ALU.mult)
-            nc.sync.dma_start(out[P * n : P * (n + 1), :], outs[n % 2][:])
+            picked = shared.tile([P, S], F32, name=f"picked_y{n}", offset=PICKED_AT[n] * KB)
+            window = out_windows[n % 2]
+            nc.vector.tensor_copy(picked[:], ys[n][:].indirect(lists[2][:]))
+            nc.vector.tensor_scalar(picked[:], picked[:], caps[:, n : n + 1], None, ALU.min)
+            nc.vector.tensor_tensor(window[:].indirect(lists[3][:]), picked[:], wgo_sb[:], ALU.mult)
+            nc.sync.dma_start(out[P * n : P * (n + 1), :], window[:])

@@ -27,7 +27,8 @@ ROW_BUFS = 5
 
 TABLE_AT = (0, 16, 32)
 WB_RAW_AT, WB_BF16_AT, TABLE_SCALES_AT = 48, 64, 72
-H_AT = {1: 52, 2: 48, 3: 56, 4: 60, 5: 32, 6: 36, 7: 40}
+H_AT = (48, 52, 48, 54, 48, 54, 48, 56)
+Z_CODES_AT = (54, 48, 56, 58)
 Z_TURNED_AT = (0, 16)
 Z_LINED_AT = (64, 0)
 OUT1_AT = 8
@@ -154,18 +155,15 @@ def tile_list_pharmacy_slot_orders_kernel(
                 picked_w[1][:, half_cols(half)], table[1][:].bitcast(U32).indirect(half_list(lists[0], half))
             )
 
-        def first_stage(j):
-            if j == 0:
-                h = held.tile([P, S], F32, name="h0")
-            else:
-                h = shared.tile([P, S], F32, name=f"h{j}", offset=H_AT[j] * KB)
+        def multiply(j):
             piece = [i for i, (c0, c1) in enumerate(WB_PIECES) if c0 <= P * j < c1][0]
             wb_cols = slice(P * j - WB_PIECES[piece][0], P * (j + 1) - WB_PIECES[piece][0])
             late = int(P * j >= EARLY)
             wh_col = P * j - late * EARLY
+            sums = []
             for half in range(2):
                 js = half_cols(half)
-                d = psum_bank(f"d{j}_{half}", 4 + (2 * j + half) % 4)
+                d = psum_bank(f"d{j}_{half}", (6 if j == 1 else 4) + half)
                 nc.tensor.matmul_mx(
                     d[:],
                     lhsT=wb_codes[piece][:, wb_cols].bitcast(FP8X4),
@@ -185,7 +183,13 @@ def tile_list_pharmacy_slot_orders_kernel(
                         start=False,
                         stop=(a == 1),
                     )
-                nc.scalar.activation(h[:, js], d[:], ACT.Tanh)
+                sums.append(d)
+            return sums
+
+        def activate(j, sums):
+            h = shared.tile([P, S], F32, name=f"h{j}", offset=H_AT[j] * KB)
+            for half in range(2):
+                nc.scalar.activation(h[:, half_cols(half)], sums[half][:], ACT.Tanh)
             scaled = h[:, BANK:S] if j == 0 else h[:]
             nc.scalar.activation(scaled, scaled, ACT.Copy, scale=gains[:, j : j + 1])
             return h
@@ -262,7 +266,7 @@ def tile_list_pharmacy_slot_orders_kernel(
                 parts = [shared.tile([P, 4 * BANK], BF16, name=f"z_lined{a}_{c}", offset=at, align_bytes=64)]
                 halves = [parts[0][:, 2 * BANK * i : 2 * BANK * (i + 1)] for i in range(2)]
             for half in range(2):
-                bank = psum_bank(f"zback{a}_{c}_{half}", 4 * (1 - a) + (2 * c + half) % 4)
+                bank = psum_bank(f"zback{a}_{c}_{half}", 6 + half if a == 0 else (2 * c + half) % 4)
                 view = bank[:].rearrange("p (b u t) -> p b u t", b=2, u=2)
                 for b in range(2):
                     for u in range(2):
@@ -272,9 +276,9 @@ def tile_list_pharmacy_slot_orders_kernel(
             z_lined[a, c] = parts
 
         def quantise_z(a, c):
-            if a == 0 and c >= 2:
+            if a == 0:
                 codes = shared.tile(
-                    [P, BANK], U32, name=f"z_codes{a}_{c}", offset=(H_AT[7] + 2 * (c - 2)) * KB, align_bytes=64
+                    [P, BANK], U32, name=f"z_codes{a}_{c}", offset=Z_CODES_AT[c] * KB, align_bytes=64
                 )
             else:
                 codes = held.tile([P, BANK], U32, name=f"z_codes{a}_{c}", align_bytes=64)
@@ -300,21 +304,31 @@ def tile_list_pharmacy_slot_orders_kernel(
                 stop=(a == 1),
             )
 
-        hs = [first_stage(0)]
+        hs = [activate(0, multiply(0))]
         place(0, hs[0])
+        hs.append(activate(1, multiply(1)))
+        banks = open_sum(0, 0)
         quantise_wb(1)
-        hs.extend(first_stage(j) for j in (1, 2))
-        quantise_wb(2)
-        hs.append(first_stage(3))
+        sums = multiply(2)
 
         scalar_only = ("scalar",) * 4
-        for j in range(5):
-            banks = open_sum(j, 0)
+        ysum = [psum_bank(f"ysum0_{c}", 4 + c) for c in range(4)]
+        for j in range(7):
             place(j + 1, hs[j + 1])
+            if j == 0:
+                quantise_wb(2)
+            if j < 6:
+                hs.append(activate(j + 2, sums))
             close_sum(j, banks, scalar_only)
-            if j < 3:
-                hs.append(first_stage(j + 4))
-            if j == 2:
+            if j < 5:
+                sums = multiply(j + 3)
+            if j in (3, 4):
+                for c in (2 * j - 6, 2 * j - 5):
+                    turn_back(0, c, scalar_only)
+            banks = open_sum(j + 1, 0)
+            if j >= 4:
+                quantise_z(0, j - 4)
+            if j == 1:
                 nc.sync.dma_start(wo_w[:], wo_words.rearrange("a p c i -> p a (c i)").bitcast(I32))
                 load_scale_rows(wo_sc, wo_scales.bitcast(I32))
                 nc.sync.dma_start(lists[2][:], offs3)
@@ -324,25 +338,10 @@ def tile_list_pharmacy_slot_orders_kernel(
                 caps = held.tile([P, 3], F32, name="caps")
                 with nc.allow_non_contiguous_dma(reason="one cap to a partition"):
                     nc.sync.dma_start(caps[:], cap.rearrange("(n p) -> p n", p=P))
-            if j == 3:
-                for c in range(4):
-                    turn_back(0, c, scalar_only)
-                    if c < 2:
-                        quantise_z(0, c)
-                hs.append(first_stage(7))
-
-        banks5 = open_sum(5, 0)
-        banks6 = open_sum(6, 4)
-        place(6, hs[6])
-        close_sum(5, banks5, scalar_only)
-        place(7, hs[7])
-        for c in (2, 3):
-            quantise_z(0, c)
-        close_sum(6, banks6, scalar_only)
-        ysum = [psum_bank(f"ysum0_{c}", 4 + c) for c in range(4)]
+        quantise_z(0, 3)
         for c in (0, 1):
             second_stage(ysum[c], 0, c, 0)
-        banks7 = open_sum(7, 0)
+        banks7 = banks
 
         close_sum(7, banks7, ("scalar", "scalar", "vector", "scalar"))
         ys = [ring.tile([P, T2], F32, name="y", tag="row", bufs=ROW_BUFS) for n in range(3)]

@@ -21,7 +21,7 @@ KB = 1024
 FLOPS = 2 * (1536 * H * S + H * N * T2)
 
 EARLY = 256
-WB_PIECES = ((0, 256), (256, 512), (512, 1024))
+WB_PIECES = ((0, 128), (128, 256), (256, 512), (512, 1024))
 PAGES = 3
 ROW_BUFS = 5
 
@@ -31,8 +31,9 @@ H_AT = (48, 52, 48, 54, 48, 54, 48, 56)
 Z_CODES_AT = (54, 48, 56, 58)
 Z_TURNED_AT = (0, 16)
 Z_LINED_AT = (64, 0)
-OUT1_AT = 8
+OUT1_AT = 40
 PICKED_AT = (44, 56, 60)
+ROWS_AT = 80
 
 
 def tile_list_pharmacy_slot_orders_kernel(
@@ -43,11 +44,13 @@ def tile_list_pharmacy_slot_orders_kernel(
     with ExitStack() as ctx:
         held = ctx.enter_context(tc.tile_pool(name="held", bufs=1))
         shared = ctx.enter_context(tc.tile_pool(name="shared", bufs=1))
-        ring = ctx.enter_context(tc.tile_pool(name="ring", bufs=1))
         psum = ctx.enter_context(tc.psum_pool(name="psum", bufs=1))
 
         def psum_bank(name, number):
             return psum.tile([P, BANK], F32, name=name, offset=2 * KB * number)
+
+        def row_slot(turn_number):
+            return (ROWS_AT + 8 * (turn_number % ROW_BUFS)) * KB
 
         def half_cols(half):
             return slice(BANK * half, BANK * (half + 1))
@@ -86,9 +89,9 @@ def tile_list_pharmacy_slot_orders_kernel(
         def load_table(a):
             nc.sync.dma_start(table[a][:], tab_words[a].rearrange("p t i -> p (t i)").bitcast(I32))
 
-        def load_scale_rows(planes, scales):
+        def load_scale_rows(queue, planes, scales):
             for q in range(4):
-                nc.sync.dma_start(
+                queue.dma_start(
                     planes[32 * q : 32 * q + 4, :, :].bitcast(I32),
                     scales[:, 4 * q : 4 * q + 4, :].rearrange("a r c -> r a c"),
                 )
@@ -131,15 +134,16 @@ def tile_list_pharmacy_slot_orders_kernel(
             nc.sync.dma_start(table_sc[1][32 * q : 32 * q + 4, :].bitcast(I32), ts32[1, 4 * q : 4 * q + 4, :])
         load_wb(0)
         load_table(1)
+        load_wb(1)
         nc.sync.dma_start(wh_w[0][:].bitcast(I32), wh32[:, :, 0 : EARLY // 2])
-        load_scale_rows(wh_sc[0], whs32[:, :, 0 : EARLY // 4])
+        load_scale_rows(nc.gpsimd, wh_sc[0], whs32[:, :, 0 : EARLY // 4])
         wgs_sb = held.tile([P, S], F32, name="wgs_sb")
         for half in range(2):
             nc.sync.dma_start(wgs_sb[:, half_cols(half)], wgs[:, half_cols(half)])
-        load_wb(1)
-        nc.sync.dma_start(wh_w[1][:].bitcast(I32), wh32[:, :, EARLY // 2 : H // 2])
-        load_scale_rows(wh_sc[1], whs32[:, :, EARLY // 4 : H // 4])
         load_wb(2)
+        nc.sync.dma_start(wh_w[1][:].bitcast(I32), wh32[:, :, EARLY // 2 : H // 2])
+        load_scale_rows(nc.sync, wh_sc[1], whs32[:, :, EARLY // 4 : H // 4])
+        load_wb(3)
 
         gains = held.tile([P, 8], F32, name="gains")
         gain_turned = psum_bank("gain_turned", 0)
@@ -154,6 +158,8 @@ def tile_list_pharmacy_slot_orders_kernel(
             nc.vector.tensor_copy(
                 picked_w[1][:, half_cols(half)], table[1][:].bitcast(U32).indirect(half_list(lists[0], half))
             )
+
+        quantise_wb(1)
 
         def multiply(j):
             piece = [i for i, (c0, c1) in enumerate(WB_PIECES) if c0 <= P * j < c1][0]
@@ -233,7 +239,7 @@ def tile_list_pharmacy_slot_orders_kernel(
                 )
 
         def open_sum(j, first_bank):
-            stock_sb = ring.tile([P, T2], F32, name="stock_sb", tag="row", bufs=ROW_BUFS)
+            stock_sb = shared.tile([P, T2], F32, name=f"stock{j}", offset=row_slot(j))
             nc.sync.dma_start(stock_sb[:], stock[P * j : P * (j + 1), :])
             banks = [psum_bank(f"zsum{j}_{c}", first_bank + c) for c in range(4)]
             for c in range(4):
@@ -308,7 +314,7 @@ def tile_list_pharmacy_slot_orders_kernel(
         place(0, hs[0])
         hs.append(activate(1, multiply(1)))
         banks = open_sum(0, 0)
-        quantise_wb(1)
+        quantise_wb(2)
         sums = multiply(2)
 
         scalar_only = ("scalar",) * 4
@@ -316,7 +322,7 @@ def tile_list_pharmacy_slot_orders_kernel(
         for j in range(7):
             place(j + 1, hs[j + 1])
             if j == 0:
-                quantise_wb(2)
+                quantise_wb(3)
             if j < 6:
                 hs.append(activate(j + 2, sums))
             close_sum(j, banks, scalar_only)
@@ -330,7 +336,7 @@ def tile_list_pharmacy_slot_orders_kernel(
                 quantise_z(0, j - 4)
             if j == 1:
                 nc.sync.dma_start(wo_w[:], wo_words.rearrange("a p c i -> p a (c i)").bitcast(I32))
-                load_scale_rows(wo_sc, wo_scales.bitcast(I32))
+                load_scale_rows(nc.sync, wo_sc, wo_scales.bitcast(I32))
                 nc.sync.dma_start(lists[2][:], offs3)
                 nc.sync.dma_start(lists[3][:], offs4)
                 wgo_sb = held.tile([P, S], F32, name="wgo_sb")
@@ -344,7 +350,7 @@ def tile_list_pharmacy_slot_orders_kernel(
         banks7 = banks
 
         close_sum(7, banks7, ("scalar", "scalar", "vector", "scalar"))
-        ys = [ring.tile([P, T2], F32, name="y", tag="row", bufs=ROW_BUFS) for n in range(3)]
+        ys = [shared.tile([P, T2], F32, name=f"y{n}", offset=row_slot(8 + n)) for n in range(3)]
         for c in range(4):
             turn_back(1, c, ("scalar" if c == 2 else "vector", "scalar"))
             quantise_z(1, c)
@@ -357,9 +363,7 @@ def tile_list_pharmacy_slot_orders_kernel(
             c0, c1 = i * BANK // 2, (i + 1) * BANK // 2
             for a in range(2):
                 second_stage(bank, 0, 3, a, c0, c1)
-            nc.scalar.copy(ys[0][:, 3 * BANK + c0 : 3 * BANK + c1], bank[:, c0:c1])
-        out_windows.append(shared.tile([P, T2], F32, name="out1", offset=OUT1_AT * KB))
-        nc.vector.memset(out_windows[1][:].bitcast(I32), 0)
+            nc.vector.tensor_copy(ys[0][:, 3 * BANK + c0 : 3 * BANK + c1], bank[:, c0:c1])
         for n in range(1, 3):
             for c in range(4):
                 bank = psum_bank(f"ysum{n}_{c}", (4 * (n - 1) + c + 1) % 8)
@@ -367,10 +371,28 @@ def tile_list_pharmacy_slot_orders_kernel(
                     second_stage(bank, n, c, a)
                 nc.scalar.copy(ys[n][:, BANK * c : BANK * (c + 1)], bank[:])
 
-        for n in range(3):
-            picked = shared.tile([P, S], F32, name=f"picked_y{n}", offset=PICKED_AT[n] * KB)
+        picked = [shared.tile([P, S], F32, name=f"picked_y{n}", offset=PICKED_AT[n] * KB) for n in range(3)]
+        capped = [shared.tile([P, S], F32, name="capped0", offset=32 * KB), shared.tile([P, S], F32, name="capped1", offset=row_slot(10)), picked[2]]
+
+        def pick(n):
+            nc.vector.tensor_copy(picked[n][:], ys[n][:].indirect(lists[2][:]))
+
+        def limit(n):
+            nc.vector.tensor_scalar(capped[n][:], picked[n][:], caps[:, n : n + 1], None, ALU.min)
+
+        def put(n):
             window = out_windows[n % 2]
-            nc.vector.tensor_copy(picked[:], ys[n][:].indirect(lists[2][:]))
-            nc.vector.tensor_scalar(picked[:], picked[:], caps[:, n : n + 1], None, ALU.min)
-            nc.vector.tensor_tensor(window[:].indirect(lists[3][:]), picked[:], wgo_sb[:], ALU.mult)
+            nc.vector.tensor_tensor(window[:].indirect(lists[3][:]), capped[n][:], wgo_sb[:], ALU.mult)
             nc.sync.dma_start(out[P * n : P * (n + 1), :], window[:])
+
+        pick(0)
+        limit(0)
+        out_windows.append(shared.tile([P, T2], F32, name="out1", offset=OUT1_AT * KB))
+        nc.gpsimd.memset(out_windows[1][:].bitcast(I32), 0)
+        put(0)
+        pick(1)
+        pick(2)
+        limit(1)
+        limit(2)
+        put(1)
+        put(2)

@@ -26,7 +26,11 @@ PAGES = 3
 ROW_BUFS = 5
 
 TABLE_AT = (0, 16, 32)
-WB_RAW_AT, WB_BF16_AT, TABLE_SCALES_AT = 48, 64, 72
+WB_RAW_AT, TABLE_SCALES_AT = 48, 72
+WB_BF16_AT = (64, 120, 135, 68)
+TANH1_AT = WB_BF16_AT[3]
+PAGE_AT = (144, 120, 128)
+OUT0_AT = 136
 H_AT = (48, 52, 48, 54, 48, 54, 48, 56)
 Z_CODES_AT = (54, 48, 56, 58)
 Z_TURNED_AT = (0, 16)
@@ -69,6 +73,7 @@ def tile_list_pharmacy_slot_orders_kernel(
         wo_sc = held.tile([P, 2, N], U8, name="wo_sc", align_bytes=64)
         picked_sc = [held.tile([P, S], U8, name=f"picked_sc{i}", align_bytes=64) for i in range(2)]
         picked_w = [held.tile([P, S], U32, name=f"picked_w{a}", align_bytes=64) for a in range(3)]
+        moved_sc = held.tile([P, S], U8, name="moved_sc", align_bytes=64)
         gain_rows = held.tile([P, P], F32, name="gain_rows")
         ident = held.tile([P, P], F32, name="ident")
 
@@ -77,14 +82,12 @@ def tile_list_pharmacy_slot_orders_kernel(
         nc.vector.memset(table_sc[1][:].bitcast(I32), 0)
         nc.vector.memset(wh_sc[0][:].rearrange("p a c -> p (a c)").bitcast(I32), 0)
         nc.vector.memset(wh_sc[1][:].rearrange("p a c -> p (a c)").bitcast(I32), 0)
+        nc.vector.memset(moved_sc[:].bitcast(I32), 0)
         nc.vector.memset(wo_sc[:].rearrange("p a c -> p (a c)").bitcast(I32), 0)
         make_identity(nc, ident[:])
-        pages = [held.tile([P, T2], F32, name=f"page{i}") for i in range(PAGES)]
-        out_windows = [held.tile([P, T2], F32, name="out0")]
-        for window in pages[0:2]:
-            nc.gpsimd.memset(window[:].bitcast(I32), 0)
-        for window in (pages[2], out_windows[0]):
-            nc.vector.memset(window[:].bitcast(I32), 0)
+        pages = [shared.tile([P, T2], F32, name=f"page{i}", offset=PAGE_AT[i] * KB) for i in range(PAGES)]
+        out_windows = [shared.tile([P, T2], F32, name="out0", offset=OUT0_AT * KB)]
+        nc.vector.memset(pages[0][:].bitcast(I32), 0)
 
         def load_table(a):
             nc.sync.dma_start(table[a][:], tab_words[a].rearrange("p t i -> p (t i)").bitcast(I32))
@@ -108,7 +111,7 @@ def tile_list_pharmacy_slot_orders_kernel(
             c0, c1 = WB_PIECES[piece]
             width = c1 - c0
             lined = shared.tile(
-                [P, width, 4], BF16, name=f"wb_bf16_{piece}", offset=WB_BF16_AT * KB + 8 * c0, align_bytes=64
+                [P, width, 4], BF16, name=f"wb_bf16_{piece}", offset=WB_BF16_AT[piece] * KB, align_bytes=64
             )
             nc.scalar.copy(
                 lined[:].rearrange("p (c e) i -> p c i e", e=4),
@@ -127,11 +130,12 @@ def tile_list_pharmacy_slot_orders_kernel(
         nc.sync.dma_start(lists[1][:], offs2)
         load_table(2)
         for q in range(4):
-            nc.sync.dma_start(table_sc[0][32 * q : 32 * q + 8, :].bitcast(I32), ts32[0:3:2, 4 * q : 4 * q + 4, :])
-        nc.sync.dma_start(gain_rows[0:8, :], gain.rearrange("(j p) -> j p", p=P))
+            nc.sync.dma_start(table_sc[0][32 * q : 32 * q + 4, :].bitcast(I32), ts32[0, 4 * q : 4 * q + 4, :])
+        nc.sync.dma_start(table_sc[0][16:32, :].bitcast(I32), ts32[1])
+        nc.gpsimd.dma_start(gain_rows[0:8, :], gain.rearrange("(j p) -> j p", p=P))
         load_table(0)
         for q in range(4):
-            nc.sync.dma_start(table_sc[1][32 * q : 32 * q + 4, :].bitcast(I32), ts32[1, 4 * q : 4 * q + 4, :])
+            nc.sync.dma_start(table_sc[1][32 * q + 4 : 32 * q + 8, :].bitcast(I32), ts32[2, 4 * q : 4 * q + 4, :])
         load_wb(0)
         load_table(1)
         load_wb(1)
@@ -153,6 +157,10 @@ def tile_list_pharmacy_slot_orders_kernel(
         for i, a in enumerate((2, 0)):
             nc.vector.tensor_copy(picked_w[a][:], table[a][:].bitcast(U32).indirect(lists[0][:]))
             nc.vector.tensor_copy(picked_sc[i][:], table_sc[i][:].indirect(lists[0][:]))
+        for q in range(4):
+            nc.gpsimd.dma_start(
+                moved_sc[32 * q : 32 * q + 4, :].bitcast(I32), picked_sc[0][16 + 4 * q : 20 + 4 * q, :].bitcast(I32)
+            )
         quantise_wb(0)
         for half in range(2):
             nc.vector.tensor_copy(
@@ -160,6 +168,7 @@ def tile_list_pharmacy_slot_orders_kernel(
             )
 
         quantise_wb(1)
+        nc.gpsimd.memset(pages[1][:].bitcast(I32), 0)
 
         def multiply(j):
             piece = [i for i, (c0, c1) in enumerate(WB_PIECES) if c0 <= P * j < c1][0]
@@ -175,7 +184,7 @@ def tile_list_pharmacy_slot_orders_kernel(
                     lhsT=wb_codes[piece][:, wb_cols].bitcast(FP8X4),
                     lhsT_scale=wb_sc[piece][:, wb_cols],
                     rhs=picked_w[2][:, js].bitcast(FP8X4),
-                    rhs_scale=picked_sc[0][4:P, js],
+                    rhs_scale=picked_sc[1][4:P, js],
                     start=True,
                     stop=False,
                 )
@@ -185,7 +194,7 @@ def tile_list_pharmacy_slot_orders_kernel(
                         lhsT=wh_w[late][:, a, 2 * wh_col : 2 * (wh_col + P)].bitcast(FP4X4),
                         lhsT_scale=wh_sc[late][:, a, wh_col : wh_col + P],
                         rhs=picked_w[a][:, js].bitcast(FP8X4),
-                        rhs_scale=picked_sc[a][:, js],
+                        rhs_scale=(picked_sc[0], moved_sc)[a][:, js],
                         start=False,
                         stop=(a == 1),
                     )
@@ -194,13 +203,16 @@ def tile_list_pharmacy_slot_orders_kernel(
 
         def activate(j, sums):
             h = shared.tile([P, S], F32, name=f"h{j}", offset=H_AT[j] * KB)
+            squashed = shared.tile([P, S], F32, name="tanh1", offset=TANH1_AT * KB) if j == 1 else h
             for half in range(2):
-                nc.scalar.activation(h[:, half_cols(half)], sums[half][:], ACT.Tanh)
-            scaled = h[:, BANK:S] if j == 0 else h[:]
-            nc.scalar.activation(scaled, scaled, ACT.Copy, scale=gains[:, j : j + 1])
+                nc.scalar.activation(squashed[:, half_cols(half)], sums[half][:], ACT.Tanh)
+            cols = slice(BANK if j == 0 else 0, S)
+            if j == 1:
+                quantise_wb(2)
+            nc.scalar.activation(h[:, cols], squashed[:, cols], ACT.Copy, scale=gains[:, j : j + 1])
             return h
 
-        wgs_gain = held.tile([P, BANK], F32, name="wgs_gain")
+        wgs_gain = shared.tile([P, BANK], F32, name="wgs_gain", offset=WB_BF16_AT[2] * KB)
         nc.scalar.activation(wgs_gain[:], wgs_sb[:, 0:BANK], ACT.Copy, scale=gains[:, 0:1])
 
         def place(j, h):
@@ -314,7 +326,8 @@ def tile_list_pharmacy_slot_orders_kernel(
         place(0, hs[0])
         hs.append(activate(1, multiply(1)))
         banks = open_sum(0, 0)
-        quantise_wb(2)
+        for window in (pages[2], out_windows[0]):
+            nc.gpsimd.memset(window[:].bitcast(I32), 0)
         sums = multiply(2)
 
         scalar_only = ("scalar",) * 4

@@ -27,7 +27,7 @@ ROW_BUFS = 5
 
 TABLE_AT = (0, 16, 32)
 WB_RAW_AT, TABLE_SCALES_AT = 48, 72
-WB_BF16_AT = (64, 120, 135, 68)
+WB_BF16_AT = (64, 65, 66, 68)
 TANH1_AT = WB_BF16_AT[3]
 PAGE_AT = (144, 120, 128)
 OUT0_AT = 136
@@ -87,7 +87,9 @@ def tile_list_pharmacy_slot_orders_kernel(
         make_identity(nc, ident[:])
         pages = [shared.tile([P, T2], F32, name=f"page{i}", offset=PAGE_AT[i] * KB) for i in range(PAGES)]
         out_windows = [shared.tile([P, T2], F32, name="out0", offset=OUT0_AT * KB)]
-        nc.vector.memset(pages[0][:].bitcast(I32), 0)
+        nc.gpsimd.memset(pages[2][:].bitcast(I32), 0)
+        for window in pages[0:2]:
+            nc.vector.memset(window[:].bitcast(I32), 0)
 
         def load_table(a):
             nc.sync.dma_start(table[a][:], tab_words[a].rearrange("p t i -> p (t i)").bitcast(I32))
@@ -138,6 +140,13 @@ def tile_list_pharmacy_slot_orders_kernel(
             nc.sync.dma_start(table_sc[1][32 * q + 4 : 32 * q + 8, :].bitcast(I32), ts32[2, 4 * q : 4 * q + 4, :])
         load_wb(0)
         load_table(1)
+        for i, a in enumerate((2, 0)):
+            nc.vector.tensor_copy(picked_w[a][:], table[a][:].bitcast(U32).indirect(lists[0][:]))
+            nc.vector.tensor_copy(picked_sc[i][:], table_sc[i][:].indirect(lists[0][:]))
+        for q in range(4):
+            nc.sync.dma_start(
+                moved_sc[32 * q : 32 * q + 4, :].bitcast(I32), picked_sc[0][16 + 4 * q : 20 + 4 * q, :].bitcast(I32)
+            )
         load_wb(1)
         nc.sync.dma_start(wh_w[0][:].bitcast(I32), wh32[:, :, 0 : EARLY // 2])
         load_scale_rows(nc.gpsimd, wh_sc[0], whs32[:, :, 0 : EARLY // 4])
@@ -154,13 +163,6 @@ def tile_list_pharmacy_slot_orders_kernel(
         nc.tensor.transpose(gain_turned[:, 0:P], gain_rows[:], ident[:])
         nc.scalar.activation(gains[:], gain_turned[:, 0:8], ACT.Copy)
 
-        for i, a in enumerate((2, 0)):
-            nc.vector.tensor_copy(picked_w[a][:], table[a][:].bitcast(U32).indirect(lists[0][:]))
-            nc.vector.tensor_copy(picked_sc[i][:], table_sc[i][:].indirect(lists[0][:]))
-        for q in range(4):
-            nc.gpsimd.dma_start(
-                moved_sc[32 * q : 32 * q + 4, :].bitcast(I32), picked_sc[0][16 + 4 * q : 20 + 4 * q, :].bitcast(I32)
-            )
         quantise_wb(0)
         for half in range(2):
             nc.vector.tensor_copy(
@@ -168,7 +170,7 @@ def tile_list_pharmacy_slot_orders_kernel(
             )
 
         quantise_wb(1)
-        nc.gpsimd.memset(pages[1][:].bitcast(I32), 0)
+        nc.vector.memset(out_windows[0][:].bitcast(I32), 0)
 
         def multiply(j):
             piece = [i for i, (c0, c1) in enumerate(WB_PIECES) if c0 <= P * j < c1][0]
@@ -326,8 +328,6 @@ def tile_list_pharmacy_slot_orders_kernel(
         place(0, hs[0])
         hs.append(activate(1, multiply(1)))
         banks = open_sum(0, 0)
-        for window in (pages[2], out_windows[0]):
-            nc.gpsimd.memset(window[:].bitcast(I32), 0)
         sums = multiply(2)
 
         scalar_only = ("scalar",) * 4

@@ -27,7 +27,7 @@ ROW_BUFS = 5
 
 TABLE_AT = (0, 16, 32)
 WB_RAW_AT, TABLE_SCALES_AT = 48, 72
-WB_BF16_AT = (64, 65, 66, 68)
+WB_BF16_AT = (64, 65, 136, 68)
 TANH1_AT = WB_BF16_AT[3]
 PAGE_AT = (144, 120, 128)
 OUT0_AT = 136
@@ -170,7 +170,6 @@ def tile_list_pharmacy_slot_orders_kernel(
             )
 
         quantise_wb(1)
-        nc.vector.memset(out_windows[0][:].bitcast(I32), 0)
 
         def multiply(j):
             piece = [i for i, (c0, c1) in enumerate(WB_PIECES) if c0 <= P * j < c1][0]
@@ -327,6 +326,7 @@ def tile_list_pharmacy_slot_orders_kernel(
         hs = [activate(0, multiply(0))]
         place(0, hs[0])
         hs.append(activate(1, multiply(1)))
+        nc.gpsimd.memset(out_windows[0][:].bitcast(I32), 0)
         banks = open_sum(0, 0)
         sums = multiply(2)
 
@@ -398,11 +398,19 @@ def tile_list_pharmacy_slot_orders_kernel(
             nc.vector.tensor_tensor(window[:].indirect(lists[3][:]), capped[n][:], wgo_sb[:], ALU.mult)
             nc.sync.dma_start(out[P * n : P * (n + 1), :], window[:])
 
-        pick(0)
-        limit(0)
+        for half in range(2):
+            nc.vector.tensor_copy(picked[0][:, half_cols(half)], ys[0][:].indirect(half_list(lists[2], half)))
+        for half in range(2):
+            cols = half_cols(half)
+            nc.vector.tensor_scalar(capped[0][:, cols], picked[0][:, cols], caps[:, 0:1], None, ALU.min)
         out_windows.append(shared.tile([P, T2], F32, name="out1", offset=OUT1_AT * KB))
         nc.gpsimd.memset(out_windows[1][:].bitcast(I32), 0)
-        put(0)
+        for half in range(2):
+            cols = half_cols(half)
+            nc.vector.tensor_tensor(
+                out_windows[0][:].indirect(half_list(lists[3], half)), capped[0][:, cols], wgo_sb[:, cols], ALU.mult
+            )
+        nc.sync.dma_start(out[0:P, :], out_windows[0][:])
         pick(1)
         pick(2)
         limit(1)

@@ -285,7 +285,7 @@ def tile_list_pharmacy_slot_orders_kernel(
                 parts = [shared.tile([P, 4 * BANK], BF16, name=f"z_lined{a}_{c}", offset=at, align_bytes=64)]
                 halves = [parts[0][:, 2 * BANK * i : 2 * BANK * (i + 1)] for i in range(2)]
             for half in range(2):
-                bank = psum_bank(f"zback{a}_{c}_{half}", 6 + half if a == 0 else (2 * c + half) % 4)
+                bank = psum_bank(f"zback{a}_{c}_{half}", (6 if a == 0 else (6, 0, 2, 6)[c]) + half)
                 view = bank[:].rearrange("p (b u t) -> p b u t", b=2, u=2)
                 for b in range(2):
                     for u in range(2):
@@ -331,7 +331,7 @@ def tile_list_pharmacy_slot_orders_kernel(
         sums = multiply(2)
 
         scalar_only = ("scalar",) * 4
-        ysum = [psum_bank(f"ysum0_{c}", 4 + c) for c in range(4)]
+        ysum = [psum_bank(f"ysum0_{c}", (4, 5, 0, 1)[c]) for c in range(4)]
         for j in range(7):
             place(j + 1, hs[j + 1])
             if j == 0:
@@ -372,14 +372,14 @@ def tile_list_pharmacy_slot_orders_kernel(
                 second_stage(ysum[c], 0, c, 0)
             second_stage(ysum[c], 0, c, 1)
             nc.scalar.copy(ys[0][:, BANK * c : BANK * (c + 1)], ysum[c][:])
-        for i, bank in enumerate((ysum[3], psum_bank("ysum0_last", 0))):
+        for i, bank in enumerate((ysum[3], psum_bank("ysum0_last", 2))):
             c0, c1 = i * BANK // 2, (i + 1) * BANK // 2
             for a in range(2):
                 second_stage(bank, 0, 3, a, c0, c1)
             nc.vector.tensor_copy(ys[0][:, 3 * BANK + c0 : 3 * BANK + c1], bank[:, c0:c1])
         for n in range(1, 3):
             for c in range(4):
-                bank = psum_bank(f"ysum{n}_{c}", (4 * (n - 1) + c + 1) % 8)
+                bank = psum_bank(f"ysum{n}_{c}", (4 * (n - 1) + c + 3) % 8)
                 for a in range(2):
                     second_stage(bank, n, c, a)
                 nc.scalar.copy(ys[n][:, BANK * c : BANK * (c + 1)], bank[:])

@@ -36,7 +36,8 @@ Z_CODES_AT = (54, 48, 56, 58)
 Z_TURNED_AT = (0, 16)
 Z_LINED_AT = (64, 0)
 OUT1_AT = 40
-PICKED_AT = (44, 56, 60)
+CAPPED_AT = (32, 80, 36)
+PICKED_AT = (16, 20, 44)
 ROWS_AT = 80
 
 
@@ -385,35 +386,14 @@ def tile_list_pharmacy_slot_orders_kernel(
                 nc.scalar.copy(ys[n][:, BANK * c : BANK * (c + 1)], bank[:])
 
         picked = [shared.tile([P, S], F32, name=f"picked_y{n}", offset=PICKED_AT[n] * KB) for n in range(3)]
-        capped = [shared.tile([P, S], F32, name="capped0", offset=32 * KB), shared.tile([P, S], F32, name="capped1", offset=row_slot(10)), picked[2]]
-
-        def pick(n):
+        capped = [shared.tile([P, S], F32, name=f"capped{n}", offset=CAPPED_AT[n] * KB) for n in range(3)]
+        for n in range(3):
             nc.vector.tensor_copy(picked[n][:], ys[n][:].indirect(lists[2][:]))
-
-        def limit(n):
-            nc.vector.tensor_scalar(capped[n][:], picked[n][:], caps[:, n : n + 1], None, ALU.min)
-
-        def put(n):
-            window = out_windows[n % 2]
-            nc.vector.tensor_tensor(window[:].indirect(lists[3][:]), capped[n][:], wgo_sb[:], ALU.mult)
-            nc.sync.dma_start(out[P * n : P * (n + 1), :], window[:])
-
-        for half in range(2):
-            nc.vector.tensor_copy(picked[0][:, half_cols(half)], ys[0][:].indirect(half_list(lists[2], half)))
-        for half in range(2):
-            cols = half_cols(half)
-            nc.vector.tensor_scalar(capped[0][:, cols], picked[0][:, cols], caps[:, 0:1], None, ALU.min)
+        for n, engine in enumerate((nc.gpsimd, nc.vector, nc.vector)):
+            engine.tensor_scalar(capped[n][:], picked[n][:], caps[:, n : n + 1], None, ALU.min)
         out_windows.append(shared.tile([P, T2], F32, name="out1", offset=OUT1_AT * KB))
         nc.gpsimd.memset(out_windows[1][:].bitcast(I32), 0)
-        for half in range(2):
-            cols = half_cols(half)
-            nc.vector.tensor_tensor(
-                out_windows[0][:].indirect(half_list(lists[3], half)), capped[0][:, cols], wgo_sb[:, cols], ALU.mult
-            )
-        nc.sync.dma_start(out[0:P, :], out_windows[0][:])
-        pick(1)
-        pick(2)
-        limit(1)
-        limit(2)
-        put(1)
-        put(2)
+        for turn_number, n in enumerate((1, 2, 0)):
+            window = out_windows[turn_number % 2]
+            nc.vector.tensor_tensor(window[:].indirect(lists[3][:]), capped[n][:], wgo_sb[:], ALU.mult)
+            nc.sync.dma_start(out[P * n : P * (n + 1), :], window[:])

@@ -276,6 +276,8 @@ def tile_list_pharmacy_slot_orders_kernel(
         def turn_back(a, c, engines):
             words = z_turned[a][c][:].bitcast(F32).rearrange("t (b u p) -> t b u p", b=4, u=2)
             at = (Z_LINED_AT[a] + 4 * c) * KB
+            if a == 0 and c >= 2:
+                at = (PAGE_AT[6 % PAGES] + 4 * (c - 2)) * KB
             if (a, c) == (1, 3):
                 parts = [
                     shared.tile([P, 2 * BANK], BF16, name=f"z_lined_last{i}", offset=at + 2 * KB * i, align_bytes=64)
@@ -286,7 +288,7 @@ def tile_list_pharmacy_slot_orders_kernel(
                 parts = [shared.tile([P, 4 * BANK], BF16, name=f"z_lined{a}_{c}", offset=at, align_bytes=64)]
                 halves = [parts[0][:, 2 * BANK * i : 2 * BANK * (i + 1)] for i in range(2)]
             for half in range(2):
-                bank = psum_bank(f"zback{a}_{c}_{half}", (6 if a == 0 else (6, 0, 2, 6)[c]) + half)
+                bank = psum_bank(f"zback{a}_{c}_{half}", ((6, 6, 6, 4) if a == 0 else (6, 0, 2, 6))[c] + half)
                 view = bank[:].rearrange("p (b u t) -> p b u t", b=2, u=2)
                 for b in range(2):
                     for u in range(2):
@@ -342,12 +344,15 @@ def tile_list_pharmacy_slot_orders_kernel(
             close_sum(j, banks, scalar_only)
             if j < 5:
                 sums = multiply(j + 3)
-            if j in (3, 4):
-                for c in (2 * j - 6, 2 * j - 5):
+            if j in (3, 6):
+                for c in ((0, 1), (2, 3))[j == 6]:
                     turn_back(0, c, scalar_only)
-            banks = open_sum(j + 1, 0)
-            if j >= 4:
+            if j in (4, 5):
                 quantise_z(0, j - 4)
+            if j == 6:
+                for c in (0, 1):
+                    second_stage(ysum[c], 0, c, 0)
+            banks = open_sum(j + 1, 0)
             if j == 1:
                 nc.sync.dma_start(wo_w[:], wo_words.rearrange("a p c i -> p a (c i)").bitcast(I32))
                 load_scale_rows(nc.sync, wo_sc, wo_scales.bitcast(I32))
@@ -358,9 +363,8 @@ def tile_list_pharmacy_slot_orders_kernel(
                 caps = held.tile([P, 3], F32, name="caps")
                 with nc.allow_non_contiguous_dma(reason="one cap to a partition"):
                     nc.sync.dma_start(caps[:], cap.rearrange("(n p) -> p n", p=P))
+        quantise_z(0, 2)
         quantise_z(0, 3)
-        for c in (0, 1):
-            second_stage(ysum[c], 0, c, 0)
         banks7 = banks
 
         close_sum(7, banks7, ("scalar", "scalar", "vector", "scalar"))

@@ -36,7 +36,9 @@ Z_CODES_AT = (54, 48, 56, 58)
 Z_TURNED_AT = (0, 16)
 Z_LINED_AT = (64, 0)
 OUT1_AT = 40
-CAPPED_AT = (32, 80, 36)
+CAPPED_AT = (32, 32, 36)
+WEIGHTED_AT = 56
+LOWEST = -3.4028234663852886e38
 PICKED_AT = (16, 20, 44)
 ROWS_AT = 80
 
@@ -391,13 +393,19 @@ def tile_list_pharmacy_slot_orders_kernel(
 
         picked = [shared.tile([P, S], F32, name=f"picked_y{n}", offset=PICKED_AT[n] * KB) for n in range(3)]
         capped = [shared.tile([P, S], F32, name=f"capped{n}", offset=CAPPED_AT[n] * KB) for n in range(3)]
+        weighted = shared.tile([P, S], F32, name="weighted0", offset=WEIGHTED_AT * KB)
         for n in range(3):
             nc.vector.tensor_copy(picked[n][:], ys[n][:].indirect(lists[2][:]))
-        for n, engine in enumerate((nc.gpsimd, nc.vector, nc.vector)):
-            engine.tensor_scalar(capped[n][:], picked[n][:], caps[:, n : n + 1], None, ALU.min)
+        for n in range(3):
+            nc.gpsimd.tensor_scalar(capped[n][:], picked[n][:], caps[:, n : n + 1], LOWEST, ALU.min, ALU.max)
+            if n == 0:
+                nc.gpsimd.tensor_tensor(weighted[:], capped[0][:], wgo_sb[:], ALU.mult)
         out_windows.append(shared.tile([P, T2], F32, name="out1", offset=OUT1_AT * KB))
         nc.gpsimd.memset(out_windows[1][:].bitcast(I32), 0)
-        for turn_number, n in enumerate((1, 2, 0)):
-            window = out_windows[turn_number % 2]
-            nc.vector.tensor_tensor(window[:].indirect(lists[3][:]), capped[n][:], wgo_sb[:], ALU.mult)
+        for n in range(3):
+            window = out_windows[n % 2]
+            if n == 0:
+                nc.vector.tensor_copy(window[:].indirect(lists[3][:]), weighted[:])
+            else:
+                nc.vector.tensor_tensor(window[:].indirect(lists[3][:]), capped[n][:], wgo_sb[:], ALU.mult)
             nc.sync.dma_start(out[P * n : P * (n + 1), :], window[:])

@@ -32,7 +32,8 @@ TANH1_AT = WB_BF16_AT[3]
 PAGE_AT = (144, 120, 128)
 OUT0_AT = 136
 H_AT = (48, 52, 48, 54, 48, 54, 48, 56)
-Z_CODES_AT = (54, 48, 56, 58)
+WGS_AT = 152
+Z_CODES_AT = (152, 154, 56, 58)
 Z_TURNED_AT = (0, 16)
 Z_LINED_AT = (64, 0)
 OUT1_AT = 40
@@ -153,7 +154,7 @@ def tile_list_pharmacy_slot_orders_kernel(
         load_wb(1)
         nc.sync.dma_start(wh_w[0][:].bitcast(I32), wh32[:, :, 0 : EARLY // 2])
         load_scale_rows(nc.gpsimd, wh_sc[0], whs32[:, :, 0 : EARLY // 4])
-        wgs_sb = held.tile([P, S], F32, name="wgs_sb")
+        wgs_sb = shared.tile([P, S], F32, name="wgs_sb", offset=WGS_AT * KB)
         for half in range(2):
             nc.sync.dma_start(wgs_sb[:, half_cols(half)], wgs[:, half_cols(half)])
         load_wb(2)
@@ -349,11 +350,6 @@ def tile_list_pharmacy_slot_orders_kernel(
             if j in (3, 6):
                 for c in ((0, 1), (2, 3))[j == 6]:
                     turn_back(0, c, scalar_only)
-            if j in (4, 5):
-                quantise_z(0, j - 4)
-            if j == 6:
-                for c in (0, 1):
-                    second_stage(ysum[c], 0, c, 0)
             banks = open_sum(j + 1, 0)
             if j == 1:
                 nc.sync.dma_start(wo_w[:], wo_words.rearrange("a p c i -> p a (c i)").bitcast(I32))
@@ -365,19 +361,18 @@ def tile_list_pharmacy_slot_orders_kernel(
                 caps = held.tile([P, 3], F32, name="caps")
                 with nc.allow_non_contiguous_dma(reason="one cap to a partition"):
                     nc.sync.dma_start(caps[:], cap.rearrange("(n p) -> p n", p=P))
-        quantise_z(0, 2)
-        quantise_z(0, 3)
+        for c in range(4):
+            quantise_z(0, c)
         banks7 = banks
 
-        close_sum(7, banks7, ("scalar", "scalar", "vector", "scalar"))
+        close_sum(7, banks7, scalar_only)
         ys = [shared.tile([P, T2], F32, name=f"y{n}", offset=row_slot(8 + n)) for n in range(3)]
         for c in range(4):
             turn_back(1, c, ("scalar" if c == 2 else "vector", "scalar"))
             quantise_z(1, c)
         for c in range(3):
-            if c == 2:
-                second_stage(ysum[c], 0, c, 0)
-            second_stage(ysum[c], 0, c, 1)
+            for a in range(2):
+                second_stage(ysum[c], 0, c, a)
             nc.scalar.copy(ys[0][:, BANK * c : BANK * (c + 1)], ysum[c][:])
         for i, bank in enumerate((ysum[3], psum_bank("ysum0_last", 2))):
             c0, c1 = i * BANK // 2, (i + 1) * BANK // 2

@@ -82,12 +82,12 @@ def tile_list_pharmacy_slot_orders_kernel(
         ident = held.tile([P, P], F32, name="ident")
 
         nc.vector.memset(table_sc[0][:].bitcast(I32), 0)
-        nc.vector.memset(gain_rows[:], 0.0)
+        nc.gpsimd.memset(gain_rows[:], 0.0)
         nc.vector.memset(table_sc[1][:].bitcast(I32), 0)
-        nc.vector.memset(wh_sc[0][:].rearrange("p a c -> p (a c)").bitcast(I32), 0)
-        nc.vector.memset(wh_sc[1][:].rearrange("p a c -> p (a c)").bitcast(I32), 0)
-        nc.vector.memset(moved_sc[:].bitcast(I32), 0)
-        nc.vector.memset(wo_sc[:].rearrange("p a c -> p (a c)").bitcast(I32), 0)
+        nc.gpsimd.memset(wh_sc[0][:].rearrange("p a c -> p (a c)").bitcast(I32), 0)
+        nc.gpsimd.memset(wh_sc[1][:].rearrange("p a c -> p (a c)").bitcast(I32), 0)
+        nc.gpsimd.memset(moved_sc[:].bitcast(I32), 0)
+        nc.gpsimd.memset(wo_sc[:].rearrange("p a c -> p (a c)").bitcast(I32), 0)
         make_identity(nc, ident[:])
         pages = [shared.tile([P, T2], F32, name=f"page{i}", offset=PAGE_AT[i] * KB) for i in range(PAGES)]
         out_windows = [shared.tile([P, T2], F32, name="out0", offset=OUT0_AT * KB)]

@@ -22,6 +22,7 @@ FLOPS = 2 * (1536 * H * S + H * N * T2)
 
 EARLY = 256
 WB_PIECES = ((0, 128), (128, 256), (256, 512), (512, 1024))
+FIRST = 256
 PAGES = 3
 ROW_BUFS = 5
 
@@ -60,11 +61,8 @@ def tile_list_pharmacy_slot_orders_kernel(
         def row_slot(turn_number):
             return (ROWS_AT + 8 * (turn_number % ROW_BUFS)) * KB
 
-        def half_cols(half):
-            return slice(BANK * half, BANK * (half + 1))
-
-        def half_list(offsets, half):
-            return offsets[:, 32 * half : 32 * (half + 1)]
+        def entries(offsets, j0, j1):
+            return offsets[:, j0 // 16 : j1 // 16]
 
         lists = [held.tile([P, S // 16], U16, name=f"list{i}") for i in range(4)]
         table = [shared.tile([P, T], I32, name=f"table{a}", offset=TABLE_AT[a] * KB) for a in range(3)]
@@ -151,12 +149,12 @@ def tile_list_pharmacy_slot_orders_kernel(
             nc.sync.dma_start(
                 moved_sc[32 * q : 32 * q + 4, :].bitcast(I32), picked_sc[0][16 + 4 * q : 20 + 4 * q, :].bitcast(I32)
             )
-        load_wb(1)
         nc.sync.dma_start(wh_w[0][:].bitcast(I32), wh32[:, :, 0 : EARLY // 2])
-        load_scale_rows(nc.gpsimd, wh_sc[0], whs32[:, :, 0 : EARLY // 4])
         wgs_sb = shared.tile([P, S], F32, name="wgs_sb", offset=WGS_AT * KB)
-        for half in range(2):
-            nc.sync.dma_start(wgs_sb[:, half_cols(half)], wgs[:, half_cols(half)])
+        nc.sync.dma_start(wgs_sb[:, 0:FIRST], wgs[:, 0:FIRST])
+        load_wb(1)
+        load_scale_rows(nc.gpsimd, wh_sc[0], whs32[:, :, 0 : EARLY // 4])
+        nc.sync.dma_start(wgs_sb[:, FIRST:S], wgs[:, FIRST:S])
         load_wb(2)
         nc.sync.dma_start(wh_w[1][:].bitcast(I32), wh32[:, :, EARLY // 2 : H // 2])
         load_scale_rows(nc.sync, wh_sc[1], whs32[:, :, EARLY // 4 : H // 4])
@@ -168,10 +166,8 @@ def tile_list_pharmacy_slot_orders_kernel(
         nc.scalar.activation(gains[:], gain_turned[:, 0:8], ACT.Copy)
 
         quantise_wb(0)
-        for half in range(2):
-            nc.vector.tensor_copy(
-                picked_w[1][:, half_cols(half)], table[1][:].bitcast(U32).indirect(half_list(lists[0], half))
-            )
+        for j0, j1 in ((0, FIRST), (FIRST, S)):
+            nc.vector.tensor_copy(picked_w[1][:, j0:j1], table[1][:].bitcast(U32).indirect(entries(lists[0], j0, j1)))
 
         quantise_wb(1)
 
@@ -181,11 +177,15 @@ def tile_list_pharmacy_slot_orders_kernel(
             late = int(P * j >= EARLY)
             wh_col = P * j - late * EARLY
             sums = []
-            for half in range(2):
-                js = half_cols(half)
-                d = psum_bank(f"d{j}_{half}", (6 if j == 1 else 4) + half)
+            if j == 0:
+                parts = ((4, 0, FIRST), (1, FIRST, BANK), (5, BANK, S))
+            else:
+                parts = [((6 if j == 1 else 4) + half, BANK * half, BANK * (half + 1)) for half in range(2)]
+            for number, j0, j1 in parts:
+                js = slice(j0, j1)
+                d = psum_bank(f"d{j}_{j0}", number)[:, 0 : j1 - j0]
                 nc.tensor.matmul_mx(
-                    d[:],
+                    d,
                     lhsT=wb_codes[piece][:, wb_cols].bitcast(FP8X4),
                     lhsT_scale=wb_sc[piece][:, wb_cols],
                     rhs=picked_w[2][:, js].bitcast(FP8X4),
@@ -195,7 +195,7 @@ def tile_list_pharmacy_slot_orders_kernel(
                 )
                 for a in range(2):
                     nc.tensor.matmul_mx(
-                        d[:],
+                        d,
                         lhsT=wh_w[late][:, a, 2 * wh_col : 2 * (wh_col + P)].bitcast(FP4X4),
                         lhsT_scale=wh_sc[late][:, a, wh_col : wh_col + P],
                         rhs=picked_w[a][:, js].bitcast(FP8X4),
@@ -203,29 +203,30 @@ def tile_list_pharmacy_slot_orders_kernel(
                         start=False,
                         stop=(a == 1),
                     )
-                sums.append(d)
+                sums.append((d, js))
             return sums
 
         def activate(j, sums):
             h = shared.tile([P, S], F32, name=f"h{j}", offset=H_AT[j] * KB)
             squashed = shared.tile([P, S], F32, name="tanh1", offset=TANH1_AT * KB) if j == 1 else h
-            for half in range(2):
-                nc.scalar.activation(squashed[:, half_cols(half)], sums[half][:], ACT.Tanh)
-            cols = slice(BANK if j == 0 else 0, S)
+            for d, js in sums:
+                nc.scalar.activation(squashed[:, js], d, ACT.Tanh)
             if j == 1:
                 quantise_wb(2)
+            cols = slice(BANK if j == 0 else 0, S)
             nc.scalar.activation(h[:, cols], squashed[:, cols], ACT.Copy, scale=gains[:, j : j + 1])
             return h
 
         wgs_gain = shared.tile([P, BANK], F32, name="wgs_gain", offset=WB_BF16_AT[2] * KB)
-        nc.scalar.activation(wgs_gain[:], wgs_sb[:, 0:BANK], ACT.Copy, scale=gains[:, 0:1])
+        for j0, j1 in ((0, FIRST), (FIRST, BANK)):
+            nc.scalar.activation(wgs_gain[:, j0:j1], wgs_sb[:, j0:j1], ACT.Copy, scale=gains[:, 0:1])
 
         def place(j, h):
             page = pages[j % PAGES]
             if j == 0:
-                for half, weights in enumerate((wgs_gain[:], wgs_sb[:, BANK:S])):
+                for j0, j1, weights in ((0, FIRST, wgs_gain), (FIRST, BANK, wgs_gain), (BANK, S, wgs_sb)):
                     nc.vector.tensor_tensor(
-                        page[:].indirect(half_list(lists[1], half)), h[:, half_cols(half)], weights, ALU.mult
+                        page[:].indirect(entries(lists[1], j0, j1)), h[:, j0:j1], weights[:, j0:j1], ALU.mult
                     )
             else:
                 nc.vector.tensor_tensor(page[:].indirect(lists[1][:]), h[:], wgs_sb[:], ALU.mult)

@@ -79,10 +79,20 @@ def tile_list_pharmacy_slot_orders_kernel(
         gain_rows = held.tile([P, P], F32, name="gain_rows")
         ident = held.tile([P, P], F32, name="ident")
 
-        nc.vector.memset(table_sc[0][:].bitcast(I32), 0)
-        nc.gpsimd.memset(gain_rows[:], 0.0)
-        nc.vector.memset(table_sc[1][:].bitcast(I32), 0)
+        def load_scale_rows(queue, planes, scales):
+            for q in range(4):
+                queue.dma_start(
+                    planes[32 * q : 32 * q + 4, :, :].bitcast(I32),
+                    scales[:, 4 * q : 4 * q + 4, :].rearrange("a r c -> r a c"),
+                )
+
+        whs32 = wh_scales.bitcast(I32)
         nc.gpsimd.memset(wh_sc[0][:].rearrange("p a c -> p (a c)").bitcast(I32), 0)
+        nc.gpsimd.memset(gain_rows[:], 0.0)
+        nc.gpsimd.dma_start(gain_rows[0:8, :], gain.rearrange("(j p) -> j p", p=P))
+        load_scale_rows(nc.gpsimd, wh_sc[0], whs32[:, :, 0 : EARLY // 4])
+        nc.vector.memset(table_sc[0][:].bitcast(I32), 0)
+        nc.vector.memset(table_sc[1][:].bitcast(I32), 0)
         nc.gpsimd.memset(wh_sc[1][:].rearrange("p a c -> p (a c)").bitcast(I32), 0)
         nc.gpsimd.memset(moved_sc[:].bitcast(I32), 0)
         nc.gpsimd.memset(wo_sc[:].rearrange("p a c -> p (a c)").bitcast(I32), 0)
@@ -95,13 +105,6 @@ def tile_list_pharmacy_slot_orders_kernel(
 
         def load_table(a):
             nc.sync.dma_start(table[a][:], tab_words[a].rearrange("p t i -> p (t i)").bitcast(I32))
-
-        def load_scale_rows(queue, planes, scales):
-            for q in range(4):
-                queue.dma_start(
-                    planes[32 * q : 32 * q + 4, :, :].bitcast(I32),
-                    scales[:, 4 * q : 4 * q + 4, :].rearrange("a r c -> r a c"),
-                )
 
         wb_raw, wb_codes, wb_sc = [], [], []
 
@@ -128,7 +131,6 @@ def tile_list_pharmacy_slot_orders_kernel(
             wb_sc.append(scales)
 
         ts32 = tab_scales.bitcast(I32)
-        whs32 = wh_scales.bitcast(I32)
         wh32 = wh_words.bitcast(I32).rearrange("a p c -> p a c")
         nc.sync.dma_start(lists[0][:], offs)
         nc.sync.dma_start(lists[1][:], offs2)
@@ -136,7 +138,6 @@ def tile_list_pharmacy_slot_orders_kernel(
         for q in range(4):
             nc.sync.dma_start(table_sc[0][32 * q : 32 * q + 4, :].bitcast(I32), ts32[0, 4 * q : 4 * q + 4, :])
         nc.sync.dma_start(table_sc[0][16:32, :].bitcast(I32), ts32[1])
-        nc.gpsimd.dma_start(gain_rows[0:8, :], gain.rearrange("(j p) -> j p", p=P))
         load_table(0)
         for q in range(4):
             nc.sync.dma_start(table_sc[1][32 * q + 4 : 32 * q + 8, :].bitcast(I32), ts32[2, 4 * q : 4 * q + 4, :])
@@ -153,7 +154,6 @@ def tile_list_pharmacy_slot_orders_kernel(
         wgs_sb = shared.tile([P, S], F32, name="wgs_sb", offset=WGS_AT * KB)
         nc.sync.dma_start(wgs_sb[:, 0:FIRST], wgs[:, 0:FIRST])
         load_wb(1)
-        load_scale_rows(nc.gpsimd, wh_sc[0], whs32[:, :, 0 : EARLY // 4])
         nc.sync.dma_start(wgs_sb[:, FIRST:S], wgs[:, FIRST:S])
         load_wb(2)
         nc.sync.dma_start(wh_w[1][:].bitcast(I32), wh32[:, :, EARLY // 2 : H // 2])

@@ -21,25 +21,28 @@ KB = 1024
 FLOPS = 2 * (1536 * H * S + H * N * T2)
 
 EARLY = 256
-WB_PIECES = ((0, 128), (128, 256), (256, 512), (512, 1024))
+WB_LOADS = ((0, 128), (128, 384), (384, 1024))
+WB_PIECES = ((0, 128), (128, 384), (384, 768), (768, 1024))
 FIRST = 256
 PAGES = 3
 ROW_BUFS = 5
 
 TABLE_AT = (0, 16, 32)
 WB_RAW_AT, TABLE_SCALES_AT = 48, 72
-WB_BF16_AT = (64, 65, 136, 68)
-TANH1_AT = WB_BF16_AT[3]
+WB_BF16_AT = (64, 65, 67, 70)
 PAGE_AT = (144, 120, 128)
 OUT0_AT = 136
-H_AT = (48, 52, 48, 54, 48, 54, 48, 56)
+H0_AT = (48, 50, 51)
+H_AT = (None, 156, 160, 164, 156, 160, 164, 156)
+WG_AT = (164, 168, 56)
+SUM_BANKS = ((0, 1, 2, 3), (4, 5, 0, 1), (2, 3, 4, 5), (0, 1, 2, 3), (4, 5, 0, 1), (2, 3, 4, 5), (0, 1, 2, 3), (0, 1, 2, 3))
 WGS_AT = 152
-Z_CODES_AT = (152, 154, 56, 58)
+Z_CODES_AT = (156, 158, 168, 170)
 Z_TURNED_AT = (0, 16)
 Z_LINED_AT = (64, 0)
 OUT1_AT = 40
 CAPPED_AT = (32, 32, 36)
-WEIGHTED_AT = 56
+WEIGHTED_AT = 168
 LOWEST = -3.4028234663852886e38
 PICKED_AT = (16, 20, 44)
 ROWS_AT = 80
@@ -109,7 +112,7 @@ def tile_list_pharmacy_slot_orders_kernel(
         wb_raw, wb_codes, wb_sc = [], [], []
 
         def load_wb(piece):
-            c0, c1 = WB_PIECES[piece]
+            c0, c1 = WB_LOADS[piece]
             raw = shared.tile([P, 4, c1 - c0], F32, name=f"wb_raw{piece}", offset=WB_RAW_AT * KB + 16 * c0)
             nc.sync.dma_start(raw[:], wb[:, c0:c1].rearrange("(p i) c -> p i c", i=4))
             wb_raw.append(raw)
@@ -117,12 +120,14 @@ def tile_list_pharmacy_slot_orders_kernel(
         def quantise_wb(piece):
             c0, c1 = WB_PIECES[piece]
             width = c1 - c0
+            load = [i for i, (l0, l1) in enumerate(WB_LOADS) if l0 <= c0 < l1][0]
+            l0 = WB_LOADS[load][0]
             lined = shared.tile(
                 [P, width, 4], BF16, name=f"wb_bf16_{piece}", offset=WB_BF16_AT[piece] * KB, align_bytes=64
             )
             nc.scalar.copy(
                 lined[:].rearrange("p (c e) i -> p c i e", e=4),
-                wb_raw[piece][:].rearrange("p i (c e) -> p c i e", e=4),
+                wb_raw[load][:, :, c0 - l0 : c1 - l0].rearrange("p i (c e) -> p c i e", e=4),
             )
             codes = held.tile([P, width], U32, name=f"wb_codes{piece}", align_bytes=64)
             scales = held.tile([P, width], U8, name=f"wb_sc{piece}", align_bytes=64)
@@ -152,13 +157,12 @@ def tile_list_pharmacy_slot_orders_kernel(
             )
         nc.sync.dma_start(wh_w[0][:].bitcast(I32), wh32[:, :, 0 : EARLY // 2])
         wgs_sb = shared.tile([P, S], F32, name="wgs_sb", offset=WGS_AT * KB)
-        nc.sync.dma_start(wgs_sb[:, 0:FIRST], wgs[:, 0:FIRST])
+        nc.sync.dma_start(wgs_sb[:, 0:BANK], wgs[:, 0:BANK])
         load_wb(1)
-        nc.sync.dma_start(wgs_sb[:, FIRST:S], wgs[:, FIRST:S])
-        load_wb(2)
+        nc.sync.dma_start(wgs_sb[:, BANK:S], wgs[:, BANK:S])
         nc.sync.dma_start(wh_w[1][:].bitcast(I32), wh32[:, :, EARLY // 2 : H // 2])
         load_scale_rows(nc.sync, wh_sc[1], whs32[:, :, EARLY // 4 : H // 4])
-        load_wb(3)
+        load_wb(2)
 
         gains = held.tile([P, 8], F32, name="gains")
         gain_turned = psum_bank("gain_turned", 0)
@@ -180,56 +184,55 @@ def tile_list_pharmacy_slot_orders_kernel(
             if j == 0:
                 parts = ((4, 0, FIRST), (1, FIRST, BANK), (5, BANK, S))
             else:
-                parts = [((6 if j == 1 else 4) + half, BANK * half, BANK * (half + 1)) for half in range(2)]
+                numbers = ((6, 7), (4, 5))[j - 1] if j < 3 else SUM_BANKS[j - 3][2:4]
+                parts = [(numbers[half], BANK * half, BANK * (half + 1)) for half in range(2)]
             for number, j0, j1 in parts:
                 js = slice(j0, j1)
                 d = psum_bank(f"d{j}_{j0}", number)[:, 0 : j1 - j0]
-                nc.tensor.matmul_mx(
-                    d,
-                    lhsT=wb_codes[piece][:, wb_cols].bitcast(FP8X4),
-                    lhsT_scale=wb_sc[piece][:, wb_cols],
-                    rhs=picked_w[2][:, js].bitcast(FP8X4),
-                    rhs_scale=picked_sc[1][4:P, js],
-                    start=True,
-                    stop=False,
-                )
-                for a in range(2):
+                order = (0, 1, 2) if j == 1 else (2, 0, 1)
+                for a in order:
+                    if a == 2:
+                        stationary = wb_codes[piece][:, wb_cols].bitcast(FP8X4)
+                        stationary_sc = wb_sc[piece][:, wb_cols]
+                    else:
+                        stationary = wh_w[late][:, a, 2 * wh_col : 2 * (wh_col + P)].bitcast(FP4X4)
+                        stationary_sc = wh_sc[late][:, a, wh_col : wh_col + P]
                     nc.tensor.matmul_mx(
                         d,
-                        lhsT=wh_w[late][:, a, 2 * wh_col : 2 * (wh_col + P)].bitcast(FP4X4),
-                        lhsT_scale=wh_sc[late][:, a, wh_col : wh_col + P],
+                        lhsT=stationary,
+                        lhsT_scale=stationary_sc,
                         rhs=picked_w[a][:, js].bitcast(FP8X4),
-                        rhs_scale=(picked_sc[0], moved_sc)[a][:, js],
-                        start=False,
-                        stop=(a == 1),
+                        rhs_scale=(picked_sc[0][:, js], moved_sc[:, js], picked_sc[1][4:P, js])[a],
+                        start=(a == order[0]),
+                        stop=(a == order[2]),
                     )
                 sums.append((d, js))
             return sums
 
         def activate(j, sums):
+            at = WG_AT[j] * KB if j < 3 else row_slot(j - 3)
+            weights = shared.tile([P, S], F32, name=f"wg{j}", offset=at)
+            for j0, j1 in ((0, FIRST), (FIRST, BANK), (BANK, S)) if j == 0 else ((0, S),):
+                nc.scalar.activation(weights[:, j0:j1], wgs_sb[:, j0:j1], ACT.Copy, scale=gains[:, j : j + 1])
+            if j == 0:
+                h = []
+                for i, (d, js) in enumerate(sums):
+                    part = shared.tile([P, js.stop - js.start], F32, name=f"h0_{i}", offset=H0_AT[i] * KB)
+                    nc.scalar.activation(part[:], d, ACT.Tanh)
+                    h.append((part, js))
+                return h, weights
             h = shared.tile([P, S], F32, name=f"h{j}", offset=H_AT[j] * KB)
-            squashed = shared.tile([P, S], F32, name="tanh1", offset=TANH1_AT * KB) if j == 1 else h
             for d, js in sums:
-                nc.scalar.activation(squashed[:, js], d, ACT.Tanh)
-            if j == 1:
-                quantise_wb(2)
-            cols = slice(BANK if j == 0 else 0, S)
-            nc.scalar.activation(h[:, cols], squashed[:, cols], ACT.Copy, scale=gains[:, j : j + 1])
-            return h
-
-        wgs_gain = shared.tile([P, BANK], F32, name="wgs_gain", offset=WB_BF16_AT[2] * KB)
-        for j0, j1 in ((0, FIRST), (FIRST, BANK)):
-            nc.scalar.activation(wgs_gain[:, j0:j1], wgs_sb[:, j0:j1], ACT.Copy, scale=gains[:, 0:1])
+                nc.scalar.activation(h[:, js], d, ACT.Tanh)
+            return [(h, slice(0, S))], weights
 
         def place(j, h):
             page = pages[j % PAGES]
-            if j == 0:
-                for j0, j1, weights in ((0, FIRST, wgs_gain), (FIRST, BANK, wgs_gain), (BANK, S, wgs_sb)):
-                    nc.vector.tensor_tensor(
-                        page[:].indirect(entries(lists[1], j0, j1)), h[:, j0:j1], weights[:, j0:j1], ALU.mult
-                    )
-            else:
-                nc.vector.tensor_tensor(page[:].indirect(lists[1][:]), h[:], wgs_sb[:], ALU.mult)
+            parts, weights = h
+            for part, js in parts:
+                nc.vector.tensor_tensor(
+                    page[:].indirect(entries(lists[1], js.start, js.stop)), part[:], weights[:, js], ALU.mult
+                )
 
         z_turned = [
             [
@@ -256,10 +259,10 @@ def tile_list_pharmacy_slot_orders_kernel(
                     is_transpose=True,
                 )
 
-        def open_sum(j, first_bank):
+        def open_sum(j):
             stock_sb = shared.tile([P, T2], F32, name=f"stock{j}", offset=row_slot(j))
             nc.sync.dma_start(stock_sb[:], stock[P * j : P * (j + 1), :])
-            banks = [psum_bank(f"zsum{j}_{c}", first_bank + c) for c in range(4)]
+            banks = [psum_bank(f"zsum{j}_{c}", SUM_BANKS[j][c]) for c in range(4)]
             for c in range(4):
                 turn(banks[c], stock_sb, c, True)
             return banks
@@ -334,24 +337,22 @@ def tile_list_pharmacy_slot_orders_kernel(
         place(0, hs[0])
         hs.append(activate(1, multiply(1)))
         nc.gpsimd.memset(out_windows[0][:].bitcast(I32), 0)
-        banks = open_sum(0, 0)
-        sums = multiply(2)
+        quantise_wb(2)
+        quantise_wb(3)
+        banks = open_sum(0)
+        hs.append(activate(2, multiply(2)))
 
         scalar_only = ("scalar",) * 4
         ysum = [psum_bank(f"ysum0_{c}", (4, 5, 0, 1)[c]) for c in range(4)]
         for j in range(7):
             place(j + 1, hs[j + 1])
-            if j == 0:
-                quantise_wb(3)
-            if j < 6:
-                hs.append(activate(j + 2, sums))
             close_sum(j, banks, scalar_only)
             if j < 5:
-                sums = multiply(j + 3)
+                hs.append(activate(j + 3, multiply(j + 3)))
             if j in (3, 6):
                 for c in ((0, 1), (2, 3))[j == 6]:
                     turn_back(0, c, scalar_only)
-            banks = open_sum(j + 1, 0)
+            banks = open_sum(j + 1)
             if j == 1:
                 nc.sync.dma_start(wo_w[:], wo_words.rearrange("a p c i -> p a (c i)").bitcast(I32))
                 load_scale_rows(nc.sync, wo_sc, wo_scales.bitcast(I32))

@@ -24,6 +24,7 @@ EARLY = 256
 WB_LOADS = ((0, 128), (128, 384), (384, 1024))
 WB_PIECES = ((0, 128), (128, 384), (384, 768), (768, 1024))
 FIRST = 256
+LEAD = 1280
 PAGES = 3
 ROW_BUFS = 5
 
@@ -76,9 +77,9 @@ def tile_list_pharmacy_slot_orders_kernel(
         wh_sc = [held.tile([P, 2, w], U8, name=f"wh_sc{w}", align_bytes=64) for w in widths]
         wh_w = [held.tile([P, 2, 2 * w], U8, name=f"wh_w{w}", align_bytes=64) for w in widths]
         wo_sc = held.tile([P, 2, N], U8, name="wo_sc", align_bytes=64)
-        picked_sc = [held.tile([P, S], U8, name=f"picked_sc{i}", align_bytes=64) for i in range(2)]
+        picked_sc = held.tile([P, 2, S], U8, name="picked_sc", align_bytes=64)
         picked_w = [held.tile([P, S], U32, name=f"picked_w{a}", align_bytes=64) for a in range(3)]
-        moved_sc = held.tile([P, S], U8, name="moved_sc", align_bytes=64)
+        moved_sc = held.tile([P, 2, S], U8, name="moved_sc", align_bytes=64)
         gain_rows = held.tile([P, P], F32, name="gain_rows")
         ident = held.tile([P, P], F32, name="ident")
 
@@ -90,24 +91,23 @@ def tile_list_pharmacy_slot_orders_kernel(
                 )
 
         whs32 = wh_scales.bitcast(I32)
+        nc.gpsimd.memset(table_sc[1][:].bitcast(I32), 0)
         nc.gpsimd.memset(wh_sc[0][:].rearrange("p a c -> p (a c)").bitcast(I32), 0)
         nc.gpsimd.memset(gain_rows[:], 0.0)
         nc.gpsimd.dma_start(gain_rows[0:8, :], gain.rearrange("(j p) -> j p", p=P))
-        load_scale_rows(nc.gpsimd, wh_sc[0], whs32[:, :, 0 : EARLY // 4])
         nc.vector.memset(table_sc[0][:].bitcast(I32), 0)
-        nc.vector.memset(table_sc[1][:].bitcast(I32), 0)
         nc.gpsimd.memset(wh_sc[1][:].rearrange("p a c -> p (a c)").bitcast(I32), 0)
-        nc.gpsimd.memset(moved_sc[:].bitcast(I32), 0)
+        nc.gpsimd.memset(moved_sc[:].rearrange("p a c -> p (a c)").bitcast(I32), 0)
         nc.gpsimd.memset(wo_sc[:].rearrange("p a c -> p (a c)").bitcast(I32), 0)
         make_identity(nc, ident[:])
         pages = [shared.tile([P, T2], F32, name=f"page{i}", offset=PAGE_AT[i] * KB) for i in range(PAGES)]
         out_windows = [shared.tile([P, T2], F32, name="out0", offset=OUT0_AT * KB)]
-        nc.gpsimd.memset(pages[2][:].bitcast(I32), 0)
-        for window in pages[0:2]:
-            nc.vector.memset(window[:].bitcast(I32), 0)
+        nc.vector.memset(pages[0][:].bitcast(I32), 0)
+        for window in pages[1:3]:
+            nc.gpsimd.memset(window[:].bitcast(I32), 0)
 
-        def load_table(a):
-            nc.sync.dma_start(table[a][:], tab_words[a].rearrange("p t i -> p (t i)").bitcast(I32))
+        def load_table(a, t0=0, t1=T):
+            nc.sync.dma_start(table[a][:, t0:t1], tab_words[a].rearrange("p t i -> p (t i)").bitcast(I32)[:, t0:t1])
 
         wb_raw, wb_codes, wb_sc = [], [], []
 
@@ -137,23 +137,25 @@ def tile_list_pharmacy_slot_orders_kernel(
 
         ts32 = tab_scales.bitcast(I32)
         wh32 = wh_words.bitcast(I32).rearrange("a p c -> p a c")
+        load_table(2, 0, LEAD)
         nc.sync.dma_start(lists[0][:], offs)
-        nc.sync.dma_start(lists[1][:], offs2)
-        load_table(2)
-        for q in range(4):
-            nc.sync.dma_start(table_sc[0][32 * q : 32 * q + 4, :].bitcast(I32), ts32[0, 4 * q : 4 * q + 4, :])
-        nc.sync.dma_start(table_sc[0][16:32, :].bitcast(I32), ts32[1])
+        nc.sync.dma_start(table_sc[1][0:P:8, :].bitcast(I32), ts32[1])
+        nc.sync.dma_start(table_sc[0][0:P:8, :].bitcast(I32), ts32[0])
+        nc.sync.dma_start(table_sc[0][4:P:8, :].bitcast(I32), ts32[2])
+        load_table(2, LEAD, T)
         load_table(0)
-        for q in range(4):
-            nc.sync.dma_start(table_sc[1][32 * q + 4 : 32 * q + 8, :].bitcast(I32), ts32[2, 4 * q : 4 * q + 4, :])
         load_wb(0)
+        nc.sync.dma_start(lists[1][:], offs2)
+        load_scale_rows(nc.sync, wh_sc[0], whs32[:, :, 0 : EARLY // 4])
         load_table(1)
-        for i, a in enumerate((2, 0)):
+        for i in (1, 0):
+            nc.vector.tensor_copy(picked_sc[:, i, :], table_sc[i][:].indirect(lists[0][:]))
+        for a in (2, 0):
             nc.vector.tensor_copy(picked_w[a][:], table[a][:].bitcast(U32).indirect(lists[0][:]))
-            nc.vector.tensor_copy(picked_sc[i][:], table_sc[i][:].indirect(lists[0][:]))
-        for q in range(4):
+        for r in range(4):
             nc.sync.dma_start(
-                moved_sc[32 * q : 32 * q + 4, :].bitcast(I32), picked_sc[0][16 + 4 * q : 20 + 4 * q, :].bitcast(I32)
+                moved_sc[r : r + 101 : 4].rearrange("p a c -> p (a c)").bitcast(I32),
+                picked_sc[8 * r : 8 * r + 101 : 4].rearrange("p a c -> p (a c)").bitcast(I32),
             )
         nc.sync.dma_start(wh_w[0][:].bitcast(I32), wh32[:, :, 0 : EARLY // 2])
         wgs_sb = shared.tile([P, S], F32, name="wgs_sb", offset=WGS_AT * KB)
@@ -202,7 +204,7 @@ def tile_list_pharmacy_slot_orders_kernel(
                         lhsT=stationary,
                         lhsT_scale=stationary_sc,
                         rhs=picked_w[a][:, js].bitcast(FP8X4),
-                        rhs_scale=(picked_sc[0][:, js], moved_sc[:, js], picked_sc[1][4:P, js])[a],
+                        rhs_scale=(moved_sc[:, 0, js], moved_sc[:, 1, js], moved_sc[4:P, 0, js])[a],
                         start=(a == order[0]),
                         stop=(a == order[2]),
                     )

@@ -24,7 +24,7 @@ EARLY = 256
 WB_LOADS = ((0, 128), (128, 384), (384, 1024))
 WB_PIECES = ((0, 128), (128, 384), (384, 768), (768, 1024))
 FIRST = 256
-LEAD = 1280
+LEAD = 1792
 PAGES = 3
 ROW_BUFS = 5
 
@@ -95,6 +95,7 @@ def tile_list_pharmacy_slot_orders_kernel(
         nc.gpsimd.memset(wh_sc[0][:].rearrange("p a c -> p (a c)").bitcast(I32), 0)
         nc.gpsimd.memset(gain_rows[:], 0.0)
         nc.gpsimd.dma_start(gain_rows[0:8, :], gain.rearrange("(j p) -> j p", p=P))
+        load_scale_rows(nc.gpsimd, wh_sc[0], whs32[:, :, 0 : EARLY // 4])
         nc.vector.memset(table_sc[0][:].bitcast(I32), 0)
         nc.gpsimd.memset(wh_sc[1][:].rearrange("p a c -> p (a c)").bitcast(I32), 0)
         nc.gpsimd.memset(moved_sc[:].rearrange("p a c -> p (a c)").bitcast(I32), 0)
@@ -146,14 +147,13 @@ def tile_list_pharmacy_slot_orders_kernel(
         load_table(0)
         load_wb(0)
         nc.sync.dma_start(lists[1][:], offs2)
-        load_scale_rows(nc.sync, wh_sc[0], whs32[:, :, 0 : EARLY // 4])
         load_table(1)
         for i in (1, 0):
             nc.vector.tensor_copy(picked_sc[:, i, :], table_sc[i][:].indirect(lists[0][:]))
         for a in (2, 0):
             nc.vector.tensor_copy(picked_w[a][:], table[a][:].bitcast(U32).indirect(lists[0][:]))
         for r in range(4):
-            nc.sync.dma_start(
+            nc.scalar.dma_start(
                 moved_sc[r : r + 101 : 4].rearrange("p a c -> p (a c)").bitcast(I32),
                 picked_sc[8 * r : 8 * r + 101 : 4].rearrange("p a c -> p (a c)").bitcast(I32),
             )

@@ -377,12 +377,12 @@ def tile_list_pharmacy_slot_orders_kernel(
         for c in range(3):
             for a in range(2):
                 second_stage(ysum[c], 0, c, a)
-            nc.scalar.copy(ys[0][:, BANK * c : BANK * (c + 1)], ysum[c][:])
+            copy_on("vector" if c == 2 else "scalar", ys[0][:, BANK * c : BANK * (c + 1)], ysum[c][:])
         for i, bank in enumerate((ysum[3], psum_bank("ysum0_last", 2))):
             c0, c1 = i * BANK // 2, (i + 1) * BANK // 2
             for a in range(2):
                 second_stage(bank, 0, 3, a, c0, c1)
-            nc.vector.tensor_copy(ys[0][:, 3 * BANK + c0 : 3 * BANK + c1], bank[:, c0:c1])
+            nc.scalar.copy(ys[0][:, 3 * BANK + c0 : 3 * BANK + c1], bank[:, c0:c1])
         for n in range(1, 3):
             for c in range(4):
                 bank = psum_bank(f"ysum{n}_{c}", (4 * (n - 1) + c + 3) % 8)

@@ -38,7 +38,7 @@ H_AT = (None, 156, 160, 164, 156, 160, 164, 156)
 WG_AT = (164, 168, 56)
 SUM_BANKS = ((0, 1, 2, 3), (4, 5, 0, 1), (2, 3, 4, 5), (0, 1, 2, 3), (4, 5, 0, 1), (2, 3, 4, 5), (0, 1, 2, 3), (0, 1, 2, 3))
 WGS_AT = 152
-Z_CODES_AT = (156, 158, 168, 170)
+Z_CODES_AT = (144, 148, 168, 170)
 Z_TURNED_AT = (0, 16)
 Z_LINED_AT = (64, 0)
 OUT1_AT = 40
@@ -141,8 +141,8 @@ def tile_list_pharmacy_slot_orders_kernel(
         load_table(2, 0, LEAD)
         nc.sync.dma_start(lists[0][:], offs)
         nc.sync.dma_start(table_sc[1][0:P:8, :].bitcast(I32), ts32[1])
-        nc.sync.dma_start(table_sc[0][0:P:8, :].bitcast(I32), ts32[0])
         nc.sync.dma_start(table_sc[0][4:P:8, :].bitcast(I32), ts32[2])
+        nc.sync.dma_start(table_sc[0][0:P:8, :].bitcast(I32), ts32[0])
         load_table(2, LEAD, T)
         load_table(0)
         load_wb(0)
@@ -365,7 +365,7 @@ def tile_list_pharmacy_slot_orders_kernel(
                 caps = held.tile([P, 3], F32, name="caps")
                 with nc.allow_non_contiguous_dma(reason="one cap to a partition"):
                     nc.sync.dma_start(caps[:], cap.rearrange("(n p) -> p n", p=P))
-        for c in range(4):
+        for c in (2, 3, 0, 1):
             quantise_z(0, c)
         banks7 = banks
 

@@ -24,7 +24,7 @@ EARLY = 256
 WB_LOADS = ((0, 128), (128, 384), (384, 1024))
 WB_PIECES = ((0, 128), (128, 384), (384, 768), (768, 1024))
 FIRST = 256
-LEAD = 1792
+LEAD = 1408
 PAGES = 3
 ROW_BUFS = 5
 
@@ -94,13 +94,12 @@ def tile_list_pharmacy_slot_orders_kernel(
         nc.gpsimd.memset(table_sc[1][:].bitcast(I32), 0)
         nc.gpsimd.memset(wh_sc[0][:].rearrange("p a c -> p (a c)").bitcast(I32), 0)
         nc.gpsimd.memset(gain_rows[:], 0.0)
-        nc.gpsimd.dma_start(gain_rows[0:8, :], gain.rearrange("(j p) -> j p", p=P))
+        make_identity(nc, ident[:])
         load_scale_rows(nc.gpsimd, wh_sc[0], whs32[:, :, 0 : EARLY // 4])
         nc.vector.memset(table_sc[0][:].bitcast(I32), 0)
         nc.gpsimd.memset(wh_sc[1][:].rearrange("p a c -> p (a c)").bitcast(I32), 0)
         nc.gpsimd.memset(moved_sc[:].rearrange("p a c -> p (a c)").bitcast(I32), 0)
         nc.gpsimd.memset(wo_sc[:].rearrange("p a c -> p (a c)").bitcast(I32), 0)
-        make_identity(nc, ident[:])
         pages = [shared.tile([P, T2], F32, name=f"page{i}", offset=PAGE_AT[i] * KB) for i in range(PAGES)]
         out_windows = [shared.tile([P, T2], F32, name="out0", offset=OUT0_AT * KB)]
         nc.vector.memset(pages[0][:].bitcast(I32), 0)
@@ -140,6 +139,7 @@ def tile_list_pharmacy_slot_orders_kernel(
         wh32 = wh_words.bitcast(I32).rearrange("a p c -> p a c")
         load_table(2, 0, LEAD)
         nc.sync.dma_start(lists[0][:], offs)
+        nc.sync.dma_start(gain_rows[0:8, :], gain.rearrange("(j p) -> j p", p=P))
         nc.sync.dma_start(table_sc[1][0:P:8, :].bitcast(I32), ts32[1])
         nc.sync.dma_start(table_sc[0][4:P:8, :].bitcast(I32), ts32[2])
         nc.sync.dma_start(table_sc[0][0:P:8, :].bitcast(I32), ts32[0])

from contextlib import ExitStack

import concourse.mybir as mybir
from concourse.masks import make_identity

F32 = mybir.dt.float32
BF16 = mybir.dt.bfloat16
I32 = mybir.dt.int32
U32 = mybir.dt.uint32
U16 = mybir.dt.uint16
U8 = mybir.dt.uint8
FP8X4 = mybir.dt.float8_e4m3fn_x4
FP4X4 = mybir.dt.float4_e2m1fn_x4
ACT = mybir.ActivationFunctionType
ALU = mybir.AluOpType

P = 128
T, S, H, T2, N = 4096, 1024, 1024, 2048, 384
BANK = 512
KB = 1024
FLOPS = 2 * (1536 * H * S + H * N * T2)

EARLY = 256
WB_LOADS = ((0, 128), (128, 384), (384, 1024))
WB_PIECES = ((0, 128), (128, 384), (384, 768), (768, 1024))
FIRST = 256
LEAD = 1408
PAGES = 3
ROW_BUFS = 5

TABLE_AT = (0, 16, 32)
WB_RAW_AT, TABLE_SCALES_AT = 48, 72
WB_BF16_AT = (64, 65, 67, 70)
PAGE_AT = (144, 120, 128)
OUT0_AT = 136
H0_AT = (48, 50, 51)
H_AT = (None, 156, 160, 164, 156, 160, 164, 156)
WG_AT = (164, 168, 56)
SUM_BANKS = ((0, 1, 2, 3), (4, 5, 0, 1), (2, 3, 4, 5), (0, 1, 2, 3), (4, 5, 0, 1), (2, 3, 4, 5), (0, 1, 2, 3), (0, 1, 2, 3))
WGS_AT = 152
Z_CODES_AT = (144, 148, 168, 170)
Z_TURNED_AT = (0, 16)
Z_LINED_AT = (64, 0)
OUT1_AT = 40
CAPPED_AT = (32, 32, 36)
WEIGHTED_AT = 168
LOWEST = -3.4028234663852886e38
PICKED_AT = (16, 20, 44)
ROWS_AT = 80


def tile_list_pharmacy_slot_orders_kernel(
    tc, tab_words, tab_scales, offs, wh_words, wh_scales, wb, gain, wgs, offs2, stock,
    wo_words, wo_scales, offs3, cap, wgo, offs4, out,
):
    nc = tc.nc
    with ExitStack() as ctx:
        held = ctx.enter_context(tc.tile_pool(name="held", bufs=1))
        shared = ctx.enter_context(tc.tile_pool(name="shared", bufs=1))
        psum = ctx.enter_context(tc.psum_pool(name="psum", bufs=1))

        def psum_bank(name, number):
            return psum.tile([P, BANK], F32, name=name, offset=2 * KB * number)

        def row_slot(turn_number):
            return (ROWS_AT + 8 * (turn_number % ROW_BUFS)) * KB

        def entries(offsets, j0, j1):
            return offsets[:, j0 // 16 : j1 // 16]

        lists = [held.tile([P, S // 16], U16, name=f"list{i}") for i in range(4)]
        table = [shared.tile([P, T], I32, name=f"table{a}", offset=TABLE_AT[a] * KB) for a in range(3)]
        table_sc = [
            shared.tile([P, T], U8, name=f"table_sc{i}", offset=(TABLE_SCALES_AT + 4 * i) * KB) for i in range(2)
        ]
        widths = (EARLY, H - EARLY)
        wh_sc = [held.tile([P, 2, w], U8, name=f"wh_sc{w}", align_bytes=64) for w in widths]
        wh_w = [held.tile([P, 2, 2 * w], U8, name=f"wh_w{w}", align_bytes=64) for w in widths]
        wo_sc = held.tile([P, 2, N], U8, name="wo_sc", align_bytes=64)
        picked_sc = held.tile([P, 2, S], U8, name="picked_sc", align_bytes=64)
        picked_w = [held.tile([P, S], U32, name=f"picked_w{a}", align_bytes=64) for a in range(3)]
        moved_sc = held.tile([P, 2, S], U8, name="moved_sc", align_bytes=64)
        gain_rows = held.tile([P, P], F32, name="gain_rows")
        ident = held.tile([P, P], F32, name="ident")

        def load_scale_rows(queue, planes, scales):
            for q in range(4):
                queue.dma_start(
                    planes[32 * q : 32 * q + 4, :, :].bitcast(I32),
                    scales[:, 4 * q : 4 * q + 4, :].rearrange("a r c -> r a c"),
                )

        whs32 = wh_scales.bitcast(I32)
        nc.gpsimd.memset(table_sc[1][:].bitcast(I32), 0)
        nc.gpsimd.memset(wh_sc[0][:].rearrange("p a c -> p (a c)").bitcast(I32), 0)
        nc.gpsimd.memset(gain_rows[:], 0.0)
        make_identity(nc, ident[:])
        load_scale_rows(nc.gpsimd, wh_sc[0], whs32[:, :, 0 : EARLY // 4])
        nc.vector.memset(table_sc[0][:].bitcast(I32), 0)
        nc.gpsimd.memset(wh_sc[1][:].rearrange("p a c -> p (a c)").bitcast(I32), 0)
        nc.gpsimd.memset(moved_sc[:].rearrange("p a c -> p (a c)").bitcast(I32), 0)
        nc.gpsimd.memset(wo_sc[:].rearrange("p a c -> p (a c)").bitcast(I32), 0)
        pages = [shared.tile([P, T2], F32, name=f"page{i}", offset=PAGE_AT[i] * KB) for i in range(PAGES)]
        out_windows = [shared.tile([P, T2], F32, name="out0", offset=OUT0_AT * KB)]
        nc.vector.memset(pages[0][:].bitcast(I32), 0)
        for window in pages[1:3]:
            nc.gpsimd.memset(window[:].bitcast(I32), 0)

        def load_table(a, t0=0, t1=T):
            nc.sync.dma_start(table[a][:, t0:t1], tab_words[a].rearrange("p t i -> p (t i)").bitcast(I32)[:, t0:t1])

        wb_raw, wb_codes, wb_sc = [], [], []

        def load_wb(piece):
            c0, c1 = WB_LOADS[piece]
            raw = shared.tile([P, 4, c1 - c0], F32, name=f"wb_raw{piece}", offset=WB_RAW_AT * KB + 16 * c0)
            nc.sync.dma_start(raw[:], wb[:, c0:c1].rearrange("(p i) c -> p i c", i=4))
            wb_raw.append(raw)

        def quantise_wb(piece):
            c0, c1 = WB_PIECES[piece]
            width = c1 - c0
            load = [i for i, (l0, l1) in enumerate(WB_LOADS) if l0 <= c0 < l1][0]
            l0 = WB_LOADS[load][0]
            lined = shared.tile(
                [P, width, 4], BF16, name=f"wb_bf16_{piece}", offset=WB_BF16_AT[piece] * KB, align_bytes=64
            )
            nc.scalar.copy(
                lined[:].rearrange("p (c e) i -> p c i e", e=4),
                wb_raw[load][:, :, c0 - l0 : c1 - l0].rearrange("p i (c e) -> p c i e", e=4),
            )
            codes = held.tile([P, width], U32, name=f"wb_codes{piece}", align_bytes=64)
            scales = held.tile([P, width], U8, name=f"wb_sc{piece}", align_bytes=64)
            nc.vector.quantize_mx(codes[:].bitcast(FP8X4), scales[:], lined[:].rearrange("p c i -> p (c i)"))
            wb_codes.append(codes)
            wb_sc.append(scales)

        ts32 = tab_scales.bitcast(I32)
        wh32 = wh_words.bitcast(I32).rearrange("a p c -> p a c")
        load_table(2, 0, LEAD)
        nc.sync.dma_start(lists[0][:], offs)
        nc.sync.dma_start(gain_rows[0:8, :], gain.rearrange("(j p) -> j p", p=P))
        nc.sync.dma_start(table_sc[1][0:P:8, :].bitcast(I32), ts32[1])
        nc.sync.dma_start(table_sc[0][4:P:8, :].bitcast(I32), ts32[2])
        nc.sync.dma_start(table_sc[0][0:P:8, :].bitcast(I32), ts32[0])
        load_table(2, LEAD, T)
        load_table(0)
        load_wb(0)
        nc.sync.dma_start(lists[1][:], offs2)
        load_table(1)
        for i in (1, 0):
            nc.vector.tensor_copy(picked_sc[:, i, :], table_sc[i][:].indirect(lists[0][:]))
        for a in (2, 0):
            nc.vector.tensor_copy(picked_w[a][:], table[a][:].bitcast(U32).indirect(lists[0][:]))
        for r in range(4):
            nc.scalar.dma_start(
                moved_sc[r : r + 101 : 4].rearrange("p a c -> p (a c)").bitcast(I32),
                picked_sc[8 * r : 8 * r + 101 : 4].rearrange("p a c -> p (a c)").bitcast(I32),
            )
        nc.sync.dma_start(wh_w[0][:].bitcast(I32), wh32[:, :, 0 : EARLY // 2])
        wgs_sb = shared.tile([P, S], F32, name="wgs_sb", offset=WGS_AT * KB)
        nc.sync.dma_start(wgs_sb[:, 0:BANK], wgs[:, 0:BANK])
        load_wb(1)
        nc.sync.dma_start(wgs_sb[:, BANK:S], wgs[:, BANK:S])
        nc.sync.dma_start(wh_w[1][:].bitcast(I32), wh32[:, :, EARLY // 2 : H // 2])
        load_scale_rows(nc.sync, wh_sc[1], whs32[:, :, EARLY // 4 : H // 4])
        load_wb(2)

        gains = held.tile([P, 8], F32, name="gains")
        gain_turned = psum_bank("gain_turned", 0)
        nc.tensor.transpose(gain_turned[:, 0:P], gain_rows[:], ident[:])
        nc.scalar.activation(gains[:], gain_turned[:, 0:8], ACT.Copy)

        quantise_wb(0)
        for j0, j1 in ((0, FIRST), (FIRST, S)):
            nc.vector.tensor_copy(picked_w[1][:, j0:j1], table[1][:].bitcast(U32).indirect(entries(lists[0], j0, j1)))

        quantise_wb(1)

        def multiply(j):
            piece = [i for i, (c0, c1) in enumerate(WB_PIECES) if c0 <= P * j < c1][0]
            wb_cols = slice(P * j - WB_PIECES[piece][0], P * (j + 1) - WB_PIECES[piece][0])
            late = int(P * j >= EARLY)
            wh_col = P * j - late * EARLY
            sums = []
            if j == 0:
                parts = ((4, 0, FIRST), (1, FIRST, BANK), (5, BANK, S))
            else:
                numbers = ((6, 7), (4, 5))[j - 1] if j < 3 else SUM_BANKS[j - 3][2:4]
                parts = [(numbers[half], BANK * half, BANK * (half + 1)) for half in range(2)]
            for number, j0, j1 in parts:
                js = slice(j0, j1)
                d = psum_bank(f"d{j}_{j0}", number)[:, 0 : j1 - j0]
                order = (0, 1, 2) if j == 1 else (2, 0, 1)
                for a in order:
                    if a == 2:
                        stationary = wb_codes[piece][:, wb_cols].bitcast(FP8X4)
                        stationary_sc = wb_sc[piece][:, wb_cols]
                    else:
                        stationary = wh_w[late][:, a, 2 * wh_col : 2 * (wh_col + P)].bitcast(FP4X4)
                        stationary_sc = wh_sc[late][:, a, wh_col : wh_col + P]
                    nc.tensor.matmul_mx(
                        d,
                        lhsT=stationary,
                        lhsT_scale=stationary_sc,
                        rhs=picked_w[a][:, js].bitcast(FP8X4),
                        rhs_scale=(moved_sc[:, 0, js], moved_sc[:, 1, js], moved_sc[4:P, 0, js])[a],
                        start=(a == order[0]),
                        stop=(a == order[2]),
                    )
                sums.append((d, js))
            return sums

        def activate(j, sums):
            at = WG_AT[j] * KB if j < 3 else row_slot(j - 3)
            weights = shared.tile([P, S], F32, name=f"wg{j}", offset=at)
            for j0, j1 in ((0, FIRST), (FIRST, BANK), (BANK, S)) if j == 0 else ((0, S),):
                nc.scalar.activation(weights[:, j0:j1], wgs_sb[:, j0:j1], ACT.Copy, scale=gains[:, j : j + 1])
            if j == 0:
                h = []
                for i, (d, js) in enumerate(sums):
                    part = shared.tile([P, js.stop - js.start], F32, name=f"h0_{i}", offset=H0_AT[i] * KB)
                    nc.scalar.activation(part[:], d, ACT.Tanh)
                    h.append((part, js))
                return h, weights
            h = shared.tile([P, S], F32, name=f"h{j}", offset=H_AT[j] * KB)
            for d, js in sums:
                nc.scalar.activation(h[:, js], d, ACT.Tanh)
            return [(h, slice(0, S))], weights

        def place(j, h):
            page = pages[j % PAGES]
            parts, weights = h
            for part, js in parts:
                nc.vector.tensor_tensor(
                    page[:].indirect(entries(lists[1], js.start, js.stop)), part[:], weights[:, js], ALU.mult
                )

        z_turned = [
            [
                shared.tile([P, 4 * BANK], BF16, name=f"z_turned{a}_{c}", offset=(Z_TURNED_AT[a] + 4 * c) * KB)
                for c in range(4)
            ]
            for a in range(2)
        ]

        def copy_on(engine, dst, src):
            if engine == "vector":
                nc.vector.tensor_copy(dst, src)
            else:
                nc.scalar.copy(dst, src)

        def turn(bank, src, c, opens):
            for b in range(4):
                nc.tensor.matmul(
                    bank[:, P * b : P * (b + 1)],
                    lhsT=src[:, BANK * c + P * b : BANK * c + P * (b + 1)],
                    rhs=ident[:],
                    start=(opens and b == 0),
                    stop=(not opens and b == 3),
                    is_transpose=True,
                )

        def open_sum(j):
            stock_sb = shared.tile([P, T2], F32, name=f"stock{j}", offset=row_slot(j))
            nc.sync.dma_start(stock_sb[:], stock[P * j : P * (j + 1), :])
            banks = [psum_bank(f"zsum{j}_{c}", SUM_BANKS[j][c]) for c in range(4)]
            for c in range(4):
                turn(banks[c], stock_sb, c, True)
            return banks

        def close_sum(j, banks, engines):
            a, g = divmod(j, 4)
            for c in range(4):
                turn(banks[c], pages[j % PAGES], c, False)
                dst = z_turned[a][c][:].rearrange("t (b u g q e) -> t b u g q e", b=4, u=2, g=4, e=2)
                copy_on(
                    engines[c], dst[:, :, :, g, :, :], banks[c][:].rearrange("t (b q u e) -> t b u q e", b=4, u=2, e=2)
                )

        z_codes = {}
        z_lined = {}
        z_sc = [held.tile([P, T2], U8, name=f"z_sc{a}", align_bytes=64) for a in range(2)]

        def turn_back(a, c, engines):
            words = z_turned[a][c][:].bitcast(F32).rearrange("t (b u p) -> t b u p", b=4, u=2)
            at = (Z_LINED_AT[a] + 4 * c) * KB
            if a == 0 and c >= 2:
                at = (PAGE_AT[6 % PAGES] + 4 * (c - 2)) * KB
            if (a, c) == (1, 3):
                parts = [
                    shared.tile([P, 2 * BANK], BF16, name=f"z_lined_last{i}", offset=at + 2 * KB * i, align_bytes=64)
                    for i in range(2)
                ]
                halves = [part[:] for part in parts]
            else:
                parts = [shared.tile([P, 4 * BANK], BF16, name=f"z_lined{a}_{c}", offset=at, align_bytes=64)]
                halves = [parts[0][:, 2 * BANK * i : 2 * BANK * (i + 1)] for i in range(2)]
            for half in range(2):
                bank = psum_bank(f"zback{a}_{c}_{half}", ((6, 6, 6, 4) if a == 0 else (6, 0, 2, 6))[c] + half)
                view = bank[:].rearrange("p (b u t) -> p b u t", b=2, u=2)
                for b in range(2):
                    for u in range(2):
                        nc.tensor.transpose(view[:, b, u, :], words[:, 2 * half + b, u, :], ident[:])
                dst = halves[half].bitcast(F32).rearrange("p (b t u) -> p b t u", b=2, u=2)
                copy_on(engines[half], dst, view.rearrange("p b u t -> p b t u"))
            z_lined[a, c] = parts

        def quantise_z(a, c):
            if a == 0:
                codes = shared.tile(
                    [P, BANK], U32, name=f"z_codes{a}_{c}", offset=Z_CODES_AT[c] * KB, align_bytes=64
                )
            else:
                codes = held.tile([P, BANK], U32, name=f"z_codes{a}_{c}", align_bytes=64)
            width = BANK // len(z_lined[a, c])
            for i, part in enumerate(z_lined[a, c]):
                nc.vector.quantize_mx(
                    codes[:, width * i : width * (i + 1)].bitcast(FP8X4),
                    z_sc[a][:, BANK * c + width * i : BANK * c + width * (i + 1)],
                    part[:],
                )
            z_codes[a, c] = codes

        wo_w = held.tile([P, 2, N], I32, name="wo_w", align_bytes=64)

        def second_stage(bank, n, c, a, c0=0, c1=BANK):
            nc.tensor.matmul_mx(
                bank[:, c0:c1],
                lhsT=wo_w[:, a, P * n : P * (n + 1)].bitcast(FP8X4),
                lhsT_scale=wo_sc[:, a, P * n : P * (n + 1)],
                rhs=z_codes[a, c][:, c0:c1].bitcast(FP8X4),
                rhs_scale=z_sc[a][:, BANK * c + c0 : BANK * c + c1],
                start=(a == 0),
                stop=(a == 1),
            )

        hs = [activate(0, multiply(0))]
        place(0, hs[0])
        hs.append(activate(1, multiply(1)))
        nc.gpsimd.memset(out_windows[0][:].bitcast(I32), 0)
        quantise_wb(2)
        quantise_wb(3)
        banks = open_sum(0)
        hs.append(activate(2, multiply(2)))

        scalar_only = ("scalar",) * 4
        ysum = [psum_bank(f"ysum0_{c}", (4, 5, 0, 1)[c]) for c in range(4)]
        for j in range(7):
            place(j + 1, hs[j + 1])
            close_sum(j, banks, scalar_only)
            if j < 5:
                hs.append(activate(j + 3, multiply(j + 3)))
            if j in (3, 6):
                for c in ((0, 1), (2, 3))[j == 6]:
                    turn_back(0, c, scalar_only)
            banks = open_sum(j + 1)
            if j == 1:
                nc.sync.dma_start(wo_w[:], wo_words.rearrange("a p c i -> p a (c i)").bitcast(I32))
                load_scale_rows(nc.sync, wo_sc, wo_scales.bitcast(I32))
                nc.sync.dma_start(lists[2][:], offs3)
                nc.sync.dma_start(lists[3][:], offs4)
                wgo_sb = held.tile([P, S], F32, name="wgo_sb")
                nc.sync.dma_start(wgo_sb[:], wgo)
                caps = held.tile([P, 3], F32, name="caps")
                with nc.allow_non_contiguous_dma(reason="one cap to a partition"):
                    nc.sync.dma_start(caps[:], cap.rearrange("(n p) -> p n", p=P))
        for c in (2, 3, 0, 1):
            quantise_z(0, c)
        banks7 = banks

        close_sum(7, banks7, scalar_only)
        ys = [shared.tile([P, T2], F32, name=f"y{n}", offset=row_slot(8 + n)) for n in range(3)]
        for c in range(4):
            turn_back(1, c, ("scalar" if c == 2 else "vector", "scalar"))
            quantise_z(1, c)
        for c in range(3):
            for a in range(2):
                second_stage(ysum[c], 0, c, a)
            copy_on("vector" if c == 2 else "scalar", ys[0][:, BANK * c : BANK * (c + 1)], ysum[c][:])
        for i, bank in enumerate((ysum[3], psum_bank("ysum0_last", 2))):
            c0, c1 = i * BANK // 2, (i + 1) * BANK // 2
            for a in range(2):
                second_stage(bank, 0, 3, a, c0, c1)
            nc.scalar.copy(ys[0][:, 3 * BANK + c0 : 3 * BANK + c1], bank[:, c0:c1])
        for n in range(1, 3):
            for c in range(4):
                bank = psum_bank(f"ysum{n}_{c}", (4 * (n - 1) + c + 3) % 8)
                for a in range(2):
                    second_stage(bank, n, c, a)
                nc.scalar.copy(ys[n][:, BANK * c : BANK * (c + 1)], bank[:])

        picked = [shared.tile([P, S], F32, name=f"picked_y{n}", offset=PICKED_AT[n] * KB) for n in range(3)]
        capped = [shared.tile([P, S], F32, name=f"capped{n}", offset=CAPPED_AT[n] * KB) for n in range(3)]
        weighted = shared.tile([P, S], F32, name="weighted0", offset=WEIGHTED_AT * KB)
        for n in range(3):
            nc.vector.tensor_copy(picked[n][:], ys[n][:].indirect(lists[2][:]))
        for n in range(3):
            nc.gpsimd.tensor_scalar(capped[n][:], picked[n][:], caps[:, n : n + 1], LOWEST, ALU.min, ALU.max)
            if n == 0:
                nc.gpsimd.tensor_tensor(weighted[:], capped[0][:], wgo_sb[:], ALU.mult)
        out_windows.append(shared.tile([P, T2], F32, name="out1", offset=OUT1_AT * KB))
        nc.gpsimd.memset(out_windows[1][:].bitcast(I32), 0)
        for n in range(3):
            window = out_windows[n % 2]
            if n == 0:
                nc.vector.tensor_copy(window[:].indirect(lists[3][:]), weighted[:])
            else:
                nc.vector.tensor_tensor(window[:].indirect(lists[3][:]), capped[n][:], wgo_sb[:], ALU.mult)
            nc.sync.dma_start(out[P * n : P * (n + 1), :], window[:])
